import numpy as np
import ml_dtypes


def mxq(x, axis, fmt="e4m3"):
    dtype, down = {"e4m3": (ml_dtypes.float8_e4m3fn, 7), "e5m2": (ml_dtypes.float8_e5m2, 14)}[fmt]
    v = np.moveaxis(np.asarray(x, np.float32).astype(ml_dtypes.bfloat16).astype(np.float64), axis, -1)
    blocks = v.reshape(v.shape[:-1] + (-1, 32))
    amax = np.abs(blocks).max(-1, keepdims=True)
    byte = np.maximum(np.where(amax > 0, np.frexp(amax)[1] - 1 + 127, 0) - down, 1)
    scale = np.exp2(byte - 127.0)
    codes = (blocks / scale).astype(np.float32).astype(dtype).astype(np.float64)
    return np.moveaxis((codes * scale).reshape(v.shape), -1, axis)


WIDE = False


def mx_kscale(k):
    if not WIDE:
        return np.ones(k)
    levels = np.array([10, -10, 5, -5, 0])
    if k % 512:
        return np.exp2(np.random.permutation(np.resize(levels, k // 32))).repeat(32)
    a = np.empty((k // 512, 16))
    for p in range(k // 512):
        a[p, :8] = np.random.permutation(np.resize(levels, 8))
        for g in range(8):
            far = levels[np.abs(levels - a[p, g]) >= 10]
            a[p, g + 8] = far[np.random.randint(len(far))]
    return np.exp2(a.ravel()).repeat(32)


BF16 = ml_dtypes.bfloat16


def bf(x):
    return np.asarray(x, np.float32).astype(BF16)


def f64(x):
    return np.asarray(x).astype(np.float64)


E2M1 = np.array([0.0, 0.5, 1.0, 1.5, 2.0, 3.0, 4.0, 6.0, -0.0, -0.5, -1.0, -1.5, -2.0, -3.0, -4.0, -6.0])


def pack_weight(w, fmt):
    k, n = w.shape
    w = f64(bf(w)).reshape(k // 32, 32, n)
    amax = np.abs(w).max(1)
    if fmt == "e4m3":
        byte = np.frexp(amax)[1] - 1 + 127 - 7
    else:
        mant, ex = np.frexp(amax / 6.0)
        byte = np.where(mant > 0.5, ex, ex - 1) + 127
    byte = np.clip(np.where(amax > 0, byte, 1), 1, 254)
    scaled = (w * np.exp2(127.0 - byte)[:, None, :]).reshape(k, n).astype(np.float32)
    by_word = np.ascontiguousarray(scaled.reshape(k // 512, 128, 4, n).transpose(0, 1, 3, 2))
    if fmt == "e4m3":
        words = by_word.astype(ml_dtypes.float8_e4m3fn).view(np.uint8)
    else:
        c = by_word.astype(ml_dtypes.float4_e2m1fn).view(np.uint8) & 0xF
        words = c[..., 0::2] | (c[..., 1::2] << 4)
    return np.ascontiguousarray(words), np.ascontiguousarray(byte.astype(np.uint8).reshape(k // 512, 16, n))


def unpack_weight(words, scales, fmt):
    g, p, n, _ = words.shape
    if fmt == "e4m3":
        vals = np.ascontiguousarray(words).view(ml_dtypes.float8_e4m3fn).astype(np.float64)
    else:
        nib = np.empty((g, p, n, 4), np.uint8)
        nib[..., 0::2] = words & 0xF
        nib[..., 1::2] = words >> 4
        vals = E2M1[nib]
    vals = vals * np.repeat(np.exp2(scales.astype(np.float64) - 127.0), 8, axis=1)[..., None]
    return vals.transpose(0, 1, 3, 2).reshape(g * 512, n)
def pack4(w):
    words, scales = pack_weight(w, "e2m1")
    return words.reshape(words.shape[0], 128, -1), scales


def unpack4(words, scales):
    return unpack_weight(words.reshape(words.shape[0], 128, -1, 2), scales, "e2m1")


U, E, M, D, C = 512, 1024, 2048, 1024, 1024

INTEREST = 0.2


def setup_inputs():
    r = mx_kscale(E)
    s = mx_kscale(D)
    t = mx_kscale(M)
    pool = np.random.standard_normal((D, M)) * s[:, None] * t
    cand = np.random.standard_normal((D, C)) / np.sqrt(D) / s[:, None]
    pool_words, pool_scales = pack4(pool)
    cand_words, cand_scales = pack4(cand)
    return {"pool_words": pool_words, "pool_scales": pool_scales,
            "cand_words": cand_words, "cand_scales": cand_scales,
            "covered": bf(0.5 * np.abs(np.random.standard_normal(M)) * t),
            "users": bf(np.random.standard_normal((U, E)) * r),
            "traits": bf(INTEREST * np.random.standard_normal((E, M)) / np.sqrt(E) / r[:, None] / t),
            "prior": bf(0.1 * np.random.standard_normal(M) / t)}


def reference(pool_words, pool_scales, cand_words, cand_scales, covered, users, traits, prior):
    pool = unpack4(pool_words, pool_scales)
    cand = unpack4(cand_words, cand_scales)
    sim = pool.T @ cand
    gain = np.maximum(sim - f64(covered)[:, None], 0.0)
    interest = mxq(f64(users), 1, "e4m3") @ mxq(f64(traits), 0, "e4m3")
    interest = interest + f64(prior)
    return mxq(interest, 1, "e4m3") @ mxq(gain, 0, "e4m3")

@@ -1,0 +1,350 @@
+from contextlib import ExitStack
+
+import concourse.mybir as mybir
+from concourse.masks import make_identity
+
+U, E, M, D, C = 512, 1024, 2048, 1024, 1024
+FLOPS = 2 * (D * M * C + U * E * M + U * M * C)
+
+F32 = mybir.dt.float32
+BF16 = mybir.dt.bfloat16
+I32 = mybir.dt.int32
+U32 = mybir.dt.uint32
+U8 = mybir.dt.uint8
+FP8X4 = mybir.dt.float8_e4m3fn_x4
+FP4X4 = mybir.dt.float4_e2m1fn_x4
+ACT = mybir.ActivationFunctionType
+ALU = mybir.AluOpType
+
+P = 128
+N = 512
+GROUPS = M // N
+INTEREST = 2
+
+SCHEDULE = [
+    ("B",),
+    ("P", 0,),
+    ("T", 0, "V",),
+    ("T", 1, "A",),
+    ("TI", 0, 3, "A",),
+    ("UQ", 0,),
+    ("UQ", 1,),
+    ("TI", 0, 1, "V",),
+    ("TI", 0, 0, "V",),
+    ("TI", 0, 2, "V",),
+    ("TQ", 0, 0,),
+    ("P", 2,),
+    ("TQ", 0, 1,),
+    ("P", 1,),
+    ("S", 0, 0,),
+    ("S", 0, 2,),
+    ("TI", 1, 0, "V",),
+    ("S", 2, 1,),
+    ("TI", 1, 3, "V",),
+    ("TI", 1, 1, "V",),
+    ("IL", 0, 0, 0, "V",),
+    ("TI", 1, 2, "V",),
+    ("TQ", 1, 0,),
+    ("TI", 2, 2, "V",),
+    ("TI", 2, 0, "V",),
+    ("TI", 2, 1, "V",),
+    ("TQ", 1, 1,),
+    ("TI", 3, 3, "V",),
+    ("TI", 2, 3, "V",),
+    ("TQ", 2, 0,),
+    ("IL", 0, 0, 1, "V",),
+    ("IL", 0, 2, 1, "V",),
+    ("TQ", 2, 1,),
+    ("P", 3,),
+    ("TI", 3, 0, "V",),
+    ("Q", 0, 0,),
+    ("IL", 0, 2, 0, "V",),
+    ("S", 0, 1,),
+    ("TI", 3, 1, "V",),
+    ("S", 2, 0,),
+    ("S", 1, 2,),
+    ("IL", 1, 2, 0, "V",),
+    ("TQ", 3, 0,),
+    ("S", 2, 2,),
+    ("IL", 1, 2, 1, "A",),
+    ("Q", 0, 2,),
+    ("IL", 2, 0, 0, "V",),
+    ("IL", 2, 0, 1, "V",),
+    ("TI", 3, 2, "V",),
+    ("IL", 2, 2, 1, "V",),
+    ("S", 1, 0,),
+    ("IL", 2, 2, 0, "V",),
+    ("IL", 1, 0, 0, "V",),
+    ("IL", 1, 0, 1, "V",),
+    ("S", 3, 0,),
+    ("TQ", 3, 1,),
+    ("Q", 2, 0,),
+    ("Q", 1, 2,),
+    ("Q", 1, 0,),
+    ("S", 1, 1,),
+    ("S", 3, 2,),
+    ("IL", 3, 0, 0, "V",),
+    ("Q", 2, 2,),
+    ("IL", 3, 0, 1, "V",),
+    ("O", 0, 0, True, False,),
+    ("IL", 0, 1, 1, "V",),
+    ("O", 1, 0, False, False,),
+    ("Q", 3, 0,),
+    ("IL", 3, 2, 0, "A",),
+    ("IL", 1, 1, 0, "V",),
+    ("IL", 3, 2, 1, "V",),
+    ("S", 3, 1,),
+    ("IL", 0, 1, 0, "V",),
+    ("Q", 3, 2,),
+    ("O", 2, 0, False, False,),
+    ("IL", 2, 1, 1, "A",),
+    ("IL", 1, 1, 1, "V",),
+    ("Q", 0, 1,),
+    ("IL", 2, 1, 0, "V",),
+    ("Q", 1, 1,),
+    ("IL", 3, 1, 0, "A",),
+    ("Q", 2, 1,),
+    ("O", 3, 0, False, True,),
+    ("IL", 3, 1, 1, "V",),
+    ("O", 0, 1, True, False,),
+    ("Q", 3, 1,),
+    ("O", 1, 1, False, False,),
+    ("F", 0, 0, "V",),
+    ("F", 0, 1, "A",),
+    ("F", 0, 2, "A",),
+    ("F", 0, 3, "V",),
+    ("O", 2, 1, False, False,),
+    ("O", 3, 1, False, True,),
+    ("F", 1, 0, "A",),
+    ("F", 1, 1, "V",),
+    ("F", 1, 2, "V",),
+    ("F", 1, 3, "A",),
+]
+
+
+def tile_facility_location_gain_s12_kernel(
+    tc, pool_words, pool_scales, cand_words, cand_scales, covered, users, traits, prior, out
+):
+    nc = tc.nc
+    with ExitStack() as ctx:
+        keep = ctx.enter_context(tc.tile_pool(name="keep", bufs=1))
+        psum = ctx.enter_context(tc.psum_pool(name="psum", bufs=1))
+        ctx.enter_context(tc.manual_schedule())
+
+        def sbuf(name, shape, dtype, tag=None, bufs=1):
+            return keep.tile(shape, dtype, name=name, tag=tag or name, bufs=bufs, align_bytes=64)
+
+        def copy(engine, out, in_):
+            if engine == "V":
+                nc.vector.tensor_copy(out=out, in_=in_)
+            else:
+                nc.scalar.copy(out=out, in_=in_)
+
+        free_banks = list(range(8))
+        bank_uses = []
+
+        def take_bank():
+            b = free_banks.pop(0)
+            bank_uses.append(b)
+            return b, psum.tile([P, N], F32, name="acc%d" % len(bank_uses), tag="bank%d" % b)
+
+        scale_rows = sbuf("scale_rows", [P, 2 * (M + C)], U8)
+        pool_scale_raw = scale_rows[:, : 2 * M].rearrange("p (k m) -> p k m", k=2)
+        cand_s = scale_rows[:, 2 * M :].rearrange("p (k c) -> p k c", k=2)
+        vec_raw = sbuf("vec_raw", [P, N], BF16)
+        vec_rows = sbuf("vec_rows", [P, N], F32)
+        bias = sbuf("bias", [P, 32], F32)
+        ident = sbuf("ident", [P, P], F32)
+        table_warm = sbuf("table_warm", [P, 2], F32)
+        cand_w = [sbuf("cand_w%d" % h, [P, 2, 2 * N], U8) for h in range(2)]
+        pool_raw = [sbuf("pool_raw%d" % g, [P, 2, 2 * N], U8) for g in range(GROUPS)]
+        pool_w = [sbuf("pool_w%d" % g, [P, 2, 2 * N], U8) for g in range(GROUPS)]
+        pool_s = [sbuf("pool_s%d" % g, [P, 2, N], U8) for g in range(GROUPS)]
+        users_raw = [sbuf("users_raw%d" % k, [P, 4 * N], BF16) for k in range(2)]
+        users_grouped = [sbuf("users_grouped%d" % k, [P, 4 * N], BF16) for k in range(2)]
+        users_w = [sbuf("users_w%d" % k, [P, N], U32) for k in range(2)]
+        users_s = [sbuf("users_s%d" % k, [P, N], U8) for k in range(2)]
+        traits_raw = [sbuf("traits_raw%d" % g, [P, 4, 2, N], BF16) for g in range(GROUPS)]
+        traits_w = [sbuf("traits_w%d" % g, [P, 2 * N], U32) for g in range(GROUPS)]
+        traits_s = [sbuf("traits_s%d" % g, [P, 2 * N], U8) for g in range(GROUPS)]
+        traits_grouped = {}
+        rows = {}
+        grouped = {}
+        words = {}
+        scales = {}
+        for g in range(GROUPS):
+            for h in range(3):
+                words[g, h] = sbuf("words%d_%d" % (g, h), [P, N], U32)
+                scales[g, h] = sbuf("scales%d_%d" % (g, h), [P, N], U8)
+        acc = {}
+
+        pool_words32 = pool_words.bitcast(I32).rearrange("k p n -> p k n")
+        cand_words32 = cand_words.bitcast(I32).rearrange("k p n -> p k n")
+        pool_scales32 = pool_scales.bitcast(I32).rearrange("k (q r) n -> r q k n", r=4)
+        cand_scales32 = cand_scales.bitcast(I32).rearrange("k (q r) n -> r q k n", r=4)
+
+        def load_words(dst, src, j):
+            nc.sync.dma_start(out=dst[:].bitcast(I32), in_=src[:, :, j * 256 : (j + 1) * 256])
+
+        def load_traits(g):
+            for k in range(2):
+                src = traits[k * N : (k + 1) * N, g * N : (g + 1) * N]
+                nc.sync.dma_start(out=traits_raw[g][:, :, k, :], in_=src.rearrange("(p j) m -> p j m", j=4))
+
+        def load_users(queue, k):
+            queue.dma_start(
+                out=users_raw[k][:].rearrange("p (r e) -> p r e", r=4),
+                in_=users[:, k * N : (k + 1) * N].rearrange("(r p) e -> p r e", p=P),
+            )
+
+        nc.vector.memset(scale_rows[:].bitcast(I32), 0)
+        nc.vector.memset(vec_rows[:], 0.0)
+        nc.vector.memset(table_warm[:], 0.0)
+        nc.scalar.activation(out=table_warm[:, 1:2], in_=table_warm[:, 0:1], func=ACT.Relu)
+        load_users(nc.gpsimd, 0)
+        load_users(nc.gpsimd, 1)
+        make_identity(nc, ident[:])
+        nc.sync.dma_start(out=vec_raw[0:4, :], in_=covered.rearrange("(g m) -> g m", g=4))
+        nc.sync.dma_start(out=vec_raw[32:36, :], in_=prior.rearrange("(g m) -> g m", g=4))
+        load_words(cand_w[0], cand_words32, 0)
+        load_words(pool_raw[0], pool_words32, 0)
+        for r in range(4):
+            nc.sync.dma_start(out=pool_scale_raw[r:P:32].bitcast(I32), in_=pool_scales32[r])
+        for r in range(4):
+            nc.sync.dma_start(out=cand_s[r:P:32].bitcast(I32), in_=cand_scales32[r])
+        load_traits(0)
+        load_words(pool_raw[1], pool_words32, 1)
+        load_words(cand_w[1], cand_words32, 1)
+        load_words(pool_raw[2], pool_words32, 2)
+        load_traits(1)
+        load_words(pool_raw[3], pool_words32, 3)
+        load_traits(2)
+        load_traits(3)
+
+
+        def permute_pool(g):
+            nc.vector.tensor_copy(
+                out=pool_w[g][:].bitcast(I32).rearrange("p k (t b w) -> p k t b w", t=4, w=4),
+                in_=pool_raw[g][:].bitcast(I32).rearrange("p k (b t w) -> p k t b w", t=4, w=4),
+            )
+            nc.vector.tensor_copy(
+                out=pool_s[g][:].bitcast(I32).rearrange("p k (t b w) -> p k t b w", t=4, w=2),
+                in_=pool_scale_raw[:, :, g * N : (g + 1) * N].bitcast(I32).rearrange("p k (b t w) -> p k t b w", t=4, w=2),
+            )
+
+        def make_bias():
+            nc.vector.tensor_scalar(
+                out=vec_rows[0:4, :].rearrange("g (t b i) -> g t b i", t=4, i=8),
+                in0=vec_raw[0:4, :].rearrange("g (b t i) -> g t b i", t=4, i=8),
+                scalar1=-1.0, scalar2=None, op0=ALU.mult,
+            )
+            nc.vector.tensor_copy(
+                out=vec_rows[32:36, :].rearrange("g (t b i) -> g t b i", t=4, i=8),
+                in_=vec_raw[32:36, :].rearrange("g (b t i) -> g t b i", t=4, i=8),
+            )
+            b, bank = take_bank()
+            for t in range(4):
+                nc.tensor.transpose(bank[:, t * P : (t + 1) * P], vec_rows[:, t * P : (t + 1) * P], ident[:])
+            nc.vector.tensor_copy(
+                out=bias[:].rearrange("p (t v g) -> p t v g", t=4, v=2),
+                in_=bank[:].rearrange("p (t v g) -> p t v g", t=4, g=32)[:, :, 0:2, 0:4],
+            )
+            free_banks.append(b)
+
+        def transpose_users(k, engine):
+            pairs = users_raw[k][:].bitcast(F32)
+            dst = users_grouped[k][:].bitcast(F32).rearrange("p (r x u) -> p r x u", r=4, u=2)
+            for q in range(2):
+                b, bank = take_bank()
+                for rr in range(2):
+                    r = 2 * q + rr
+                    for u in range(2):
+                        col = (2 * rr + u) * P
+                        nc.tensor.transpose(
+                            bank[:, col : col + P], pairs[:, 256 * r + u : 256 * (r + 1) : 2], ident[:]
+                        )
+                copy(engine, dst[:, 2 * q : 2 * q + 2], bank[:].rearrange("p (r u x) -> p r x u", r=2, u=2))
+                free_banks.append(b)
+
+        def quantize_users(k):
+            nc.vector.quantize_mx(out=users_w[k][:].bitcast(FP8X4), scales=users_s[k][:], in_=users_grouped[k][:])
+
+        def group_traits(g, t, engine):
+            if g not in traits_grouped:
+                traits_grouped[g] = sbuf("traits_grouped%d" % g, [P, 4, 2 * N], BF16, tag="traits_grouped", bufs=2)
+            copy(
+                engine,
+                traits_grouped[g][:, t, :].rearrange("p (b h i j) -> p b h j i", h=2, i=4, j=4),
+                traits_raw[g][:].rearrange("p j k (b t h i) -> p t (k b) h j i", t=4, h=2, i=4)[:, t],
+            )
+
+        def quantize_traits(g, half):
+            cols = slice(half * N, (half + 1) * N)
+            nc.vector.quantize_mx(
+                out=traits_w[g][:, cols].bitcast(FP8X4),
+                scales=traits_s[g][:, cols],
+                in_=traits_grouped[g][:, 2 * half : 2 * half + 2, :].rearrange("p t x -> p (t x)"),
+            )
+
+        def first_stage(g, h):
+            rows[g, h] = sbuf("rows%d_%d" % (g, h), [P, 4, N], BF16, tag="rows", bufs=8)
+            for t in range(4):
+                b, bank = take_bank()
+                for k in range(2):
+                    if h == INTEREST:
+                        cols = slice((2 * t + k) * P, (2 * t + k + 1) * P)
+                        lhsT, lhsT_scale = traits_w[g][:, cols].bitcast(FP8X4), traits_s[g][:, cols]
+                        rhs, rhs_scale = users_w[k][:].bitcast(FP8X4), users_s[k][:]
+                    else:
+                        lhsT = pool_w[g][:, k, 2 * t * P : 2 * (t + 1) * P].bitcast(FP4X4)
+                        lhsT_scale = pool_s[g][:, k, t * P : (t + 1) * P]
+                        rhs, rhs_scale = cand_w[h][:, k, :].bitcast(FP4X4), cand_s[:, k, h * N : (h + 1) * N]
+                    nc.tensor.matmul_mx(
+                        out=bank[:], lhsT=lhsT, lhsT_scale=lhsT_scale, rhs=rhs, rhs_scale=rhs_scale,
+                        start=(k == 0), stop=(k == 1),
+                    )
+                col = 8 * t + (4 if h == INTEREST else 0) + g
+                nc.scalar.activation(
+                    out=rows[g, h][:, t, :], in_=bank[:],
+                    func=ACT.Identity if h == INTEREST else ACT.Relu, bias=bias[:, col : col + 1],
+                )
+                free_banks.append(b)
+
+        def interleave(g, h, half, engine):
+            if (g, h) not in grouped:
+                grouped[g, h] = sbuf("grouped%d_%d" % (g, h), [P, 4 * N], BF16, tag="grouped", bufs=4)
+            copy(
+                engine,
+                grouped[g, h][:, half * 2 * N : (half + 1) * 2 * N].rearrange("p (c i t) -> p c t i", i=4, t=4),
+                rows[g, h][:, :, half * 256 : (half + 1) * 256].rearrange("p t (c i) -> p c t i", i=4),
+            )
+
+        def quantize_result(g, h):
+            nc.vector.quantize_mx(out=words[g, h][:].bitcast(FP8X4), scales=scales[g, h][:], in_=grouped[g, h][:])
+
+        def second_stage(g, h, first, last):
+            for r in range(4):
+                if first:
+                    acc[h, r] = take_bank()
+                cols = slice(r * P, (r + 1) * P)
+                nc.tensor.matmul_mx(
+                    out=acc[h, r][1][:],
+                    lhsT=words[g, INTEREST][:, cols].bitcast(FP8X4), lhsT_scale=scales[g, INTEREST][:, cols],
+                    rhs=words[g, h][:].bitcast(FP8X4), rhs_scale=scales[g, h][:],
+                    start=first, stop=last,
+                )
+
+        def finish(h, r, engine):
+            b, bank = acc[h, r]
+            result = sbuf("result%d_%d" % (h, r), [P, N], F32, tag="result", bufs=8)
+            copy(engine, result[:], bank[:])
+            free_banks.append(b)
+            nc.sync.dma_start(out=out[r * P : (r + 1) * P, h * N : (h + 1) * N], in_=result[:])
+
+        steps = {
+            "P": permute_pool, "B": make_bias, "T": transpose_users, "UQ": quantize_users,
+            "TI": group_traits, "TQ": quantize_traits, "S": first_stage, "IL": interleave,
+            "Q": quantize_result, "O": second_stage, "F": finish,
+        }
+        for step in SCHEDULE:
+            steps[step[0]](*step[1:])

@@ -21,104 +21,142 @@ N = 512
 GROUPS = M // N
 INTEREST = 2
 
+COLUMN_PIECES = {0: [(0, 256), (256, 512)], 1: [(0, 256), (256, 384), (384, 512)], 2: [(0, 256), (256, 512)]}
+
+TILES_PER_STORE = [1, 4, 2]
+
 SCHEDULE = [
+    ("W", 9,),
     ("B",),
+    ("W", 4,),
     ("P", 0,),
-    ("T", 0, "V",),
-    ("T", 1, "A",),
-    ("TI", 0, 3, "A",),
+    ("TK", 0, 1, "V",),
+    ("T", 0, "A",),
+    ("TK", 0, 0, "V",),
+    ("TK", 0, 3, "V",),
+    ("TK", 0, 2, "V",),
     ("UQ", 0,),
-    ("UQ", 1,),
-    ("TI", 0, 1, "V",),
-    ("TI", 0, 0, "V",),
-    ("TI", 0, 2, "V",),
-    ("TQ", 0, 0,),
-    ("P", 2,),
-    ("TQ", 0, 1,),
-    ("P", 1,),
     ("S", 0, 0,),
-    ("S", 0, 2,),
-    ("TI", 1, 0, "V",),
-    ("S", 2, 1,),
-    ("TI", 1, 3, "V",),
-    ("TI", 1, 1, "V",),
+    ("P", 2,),
+    ("IL", 0, 0, 1, "V",),
+    ("S", 0, 1,),
     ("IL", 0, 0, 0, "V",),
+    ("P", 3,),
+    ("TK", 1, 0, "V",),
+    ("P", 1,),
+    ("IL", 0, 1, 0, "V",),
+    ("TK", 1, 3, "V",),
+    ("TK", 1, 2, "V",),
+    ("TK", 1, 1, "V",),
+    ("TQ", 0, 1,),
+    ("TI", 2, 1, "V",),
+    ("TI", 2, 2, "V",),
+    ("TQ", 0, 0,),
+    ("S", 2, 0,),
+    ("TI", 2, 0, "V",),
+    ("TI", 2, 3, "V",),
+    ("S", 3, 0,),
+    ("TQ", 2, 0,),
+    ("TI", 1, 3, "V",),
+    ("TQ", 2, 1,),
+    ("S", 1, 0,),
+    ("Q", 0, 0,),
+    ("TI", 1, 1, "V",),
+    ("TI", 1, 0, "V",),
+    ("IL", 1, 0, 0, "V",),
+    ("IL", 3, 0, 1, "A",),
+    ("T", 1, "A",),
+    ("IL", 3, 0, 0, "V",),
+    ("S", 3, 1,),
+    ("TI", 3, 2, "V",),
+    ("TI", 3, 1, "V",),
+    ("S", 1, 1,),
+    ("UQ", 1,),
+    ("S", 0, 2,),
+    ("TI", 3, 0, "V",),
+    ("IL", 2, 0, 0, "V",),
     ("TI", 1, 2, "V",),
     ("TQ", 1, 0,),
-    ("TI", 2, 2, "V",),
-    ("TI", 2, 0, "V",),
-    ("TI", 2, 1, "V",),
-    ("TQ", 1, 1,),
-    ("TI", 3, 3, "V",),
-    ("TI", 2, 3, "V",),
-    ("TQ", 2, 0,),
-    ("IL", 0, 0, 1, "V",),
-    ("IL", 0, 2, 1, "V",),
-    ("TQ", 2, 1,),
-    ("P", 3,),
-    ("TI", 3, 0, "V",),
-    ("Q", 0, 0,),
-    ("IL", 0, 2, 0, "V",),
-    ("S", 0, 1,),
-    ("TI", 3, 1, "V",),
-    ("S", 2, 0,),
-    ("S", 1, 2,),
-    ("IL", 1, 2, 0, "V",),
-    ("TQ", 3, 0,),
-    ("S", 2, 2,),
-    ("IL", 1, 2, 1, "A",),
-    ("Q", 0, 2,),
-    ("IL", 2, 0, 0, "V",),
     ("IL", 2, 0, 1, "V",),
-    ("TI", 3, 2, "V",),
-    ("IL", 2, 2, 1, "V",),
-    ("S", 1, 0,),
-    ("IL", 2, 2, 0, "V",),
-    ("IL", 1, 0, 0, "V",),
-    ("IL", 1, 0, 1, "V",),
-    ("S", 3, 0,),
-    ("TQ", 3, 1,),
-    ("Q", 2, 0,),
-    ("Q", 1, 2,),
-    ("Q", 1, 0,),
-    ("S", 1, 1,),
-    ("S", 3, 2,),
-    ("IL", 3, 0, 0, "V",),
-    ("Q", 2, 2,),
-    ("IL", 3, 0, 1, "V",),
-    ("O", 0, 0, True, False,),
+    ("TQ", 3, 0,),
+    ("TQ", 1, 1,),
+    ("S", 2, 2,),
+    ("IL", 0, 2, 1, "V",),
     ("IL", 0, 1, 1, "V",),
-    ("O", 1, 0, False, False,),
+    ("S", 1, 2,),
+    ("IL", 0, 2, 0, "V",),
+    ("TI", 3, 3, "V",),
+    ("Q", 0, 2,),
+    ("IL", 1, 0, 1, "V",),
+    ("TQ", 3, 1,),
+    ("Q", 1, 0,),
+    ("QH", 0, 0,),
+    ("IL", 1, 2, 0, "V",),
+    ("Q", 2, 0,),
+    ("IL", 1, 2, 1, "V",),
+    ("S", 3, 2,),
+    ("IL", 2, 2, 1, "V",),
+    ("IL", 2, 2, 0, "A",),
+    ("IL", 3, 2, 0, "V",),
+    ("Q", 1, 2,),
+    ("IL", 3, 2, 1, "A",),
+    ("O", 0, 0, True, False,),
+    ("S", 2, 1,),
+    ("Q", 2, 2,),
+    ("IL", 0, 1, 2, "V",),
     ("Q", 3, 0,),
-    ("IL", 3, 2, 0, "A",),
-    ("IL", 1, 1, 0, "V",),
-    ("IL", 3, 2, 1, "V",),
-    ("S", 3, 1,),
-    ("IL", 0, 1, 0, "V",),
-    ("Q", 3, 2,),
+    ("O", 1, 0, False, False,),
     ("O", 2, 0, False, False,),
-    ("IL", 2, 1, 1, "A",),
-    ("IL", 1, 1, 1, "V",),
-    ("Q", 0, 1,),
-    ("IL", 2, 1, 0, "V",),
-    ("Q", 1, 1,),
     ("IL", 3, 1, 0, "A",),
-    ("Q", 2, 1,),
+    ("Q", 3, 2,),
+    ("QH", 0, 1,),
+    ("IL", 1, 1, 1, "V",),
     ("O", 3, 0, False, True,),
-    ("IL", 3, 1, 1, "V",),
-    ("O", 0, 1, True, False,),
-    ("Q", 3, 1,),
-    ("O", 1, 1, False, False,),
-    ("F", 0, 0, "V",),
+    ("IL", 1, 1, 0, "V",),
+    ("OH", 0, 0, True, False,),
+    ("F", 0, 0, "A",),
+    ("IL", 2, 1, 0, "V",),
+    ("QH", 1, 0,),
+    ("OH", 1, 0, False, False,),
+    ("QH", 2, 0,),
+    ("OH", 2, 0, False, False,),
     ("F", 0, 1, "A",),
+    ("QH", 3, 0,),
+    ("IL", 3, 1, 1, "V",),
+    ("QH", 1, 1,),
+    ("IL", 2, 1, 1, "V",),
+    ("IL", 2, 1, 2, "V",),
     ("F", 0, 2, "A",),
-    ("F", 0, 3, "V",),
-    ("O", 2, 1, False, False,),
-    ("O", 3, 1, False, True,),
-    ("F", 1, 0, "A",),
-    ("F", 1, 1, "V",),
-    ("F", 1, 2, "V",),
-    ("F", 1, 3, "A",),
+    ("OH", 3, 0, False, True,),
+    ("QH", 3, 1,),
+    ("FH", 0, 0, "A",),
+    ("OH", 0, 1, True, False,),
+    ("F", 0, 3, "A",),
+    ("OH", 1, 1, False, False,),
+    ("IL", 1, 1, 2, "V",),
+    ("QH", 2, 1,),
+    ("OH", 2, 1, False, False,),
+    ("FH", 0, 1, "V",),
+    ("FH", 0, 2, "A",),
+    ("QH", 0, 2,),
+    ("OH", 3, 1, False, True,),
+    ("FH", 0, 3, "A",),
+    ("IL", 3, 1, 2, "V",),
+    ("OH", 0, 2, True, False,),
+    ("QH", 1, 2,),
+    ("FH", 1, 0, "V",),
+    ("FH", 1, 1, "A",),
+    ("QH", 2, 2,),
+    ("OH", 1, 2, False, False,),
+    ("QH", 3, 2,),
+    ("OH", 2, 2, False, False,),
+    ("FH", 1, 2, "A",),
+    ("FH", 1, 3, "V",),
+    ("OH", 3, 2, False, True,),
+    ("FH", 2, 0, "A",),
+    ("FH", 2, 1, "V",),
+    ("FH", 2, 2, "A",),
+    ("FH", 2, 3, "V",),
 ]
 
 
@@ -148,9 +186,10 @@ def tile_facility_location_gain_s12_kernel(
             bank_uses.append(b)
             return b, psum.tile([P, N], F32, name="acc%d" % len(bank_uses), tag="bank%d" % b)
 
-        scale_rows = sbuf("scale_rows", [P, 2 * (M + C)], U8)
-        pool_scale_raw = scale_rows[:, : 2 * M].rearrange("p (k m) -> p k m", k=2)
-        cand_s = scale_rows[:, 2 * M :].rearrange("p (k c) -> p k c", k=2)
+        pool_scale_rows = sbuf("pool_scale_rows", [P, 2, N], U8)
+        later_scales = sbuf("later_scales", [P, 2, M - N], U8)
+        pool_scale_raw = [pool_scale_rows[:]] + [later_scales[:, :, g * N : (g + 1) * N] for g in range(GROUPS - 1)]
+        cand_s = sbuf("cand_s", [P, 2, C], U8)
         vec_raw = sbuf("vec_raw", [P, N], BF16)
         vec_rows = sbuf("vec_rows", [P, N], F32)
         bias = sbuf("bias", [P, 32], F32)
@@ -177,6 +216,7 @@ def tile_facility_location_gain_s12_kernel(
                 words[g, h] = sbuf("words%d_%d" % (g, h), [P, N], U32)
                 scales[g, h] = sbuf("scales%d_%d" % (g, h), [P, N], U8)
         acc = {}
+        results = {}
 
         pool_words32 = pool_words.bitcast(I32).rearrange("k p n -> p k n")
         cand_words32 = cand_words.bitcast(I32).rearrange("k p n -> p k n")
@@ -186,10 +226,9 @@ def tile_facility_location_gain_s12_kernel(
         def load_words(dst, src, j):
             nc.sync.dma_start(out=dst[:].bitcast(I32), in_=src[:, :, j * 256 : (j + 1) * 256])
 
-        def load_traits(g):
-            for k in range(2):
-                src = traits[k * N : (k + 1) * N, g * N : (g + 1) * N]
-                nc.sync.dma_start(out=traits_raw[g][:, :, k, :], in_=src.rearrange("(p j) m -> p j m", j=4))
+        def load_traits(g, k):
+            src = traits[k * N : (k + 1) * N, g * N : (g + 1) * N]
+            nc.sync.dma_start(out=traits_raw[g][:, :, k, :], in_=src.rearrange("(p j) m -> p j m", j=4))
 
         def load_users(queue, k):
             queue.dma_start(
@@ -197,30 +236,63 @@ def tile_facility_location_gain_s12_kernel(
                 in_=users[:, k * N : (k + 1) * N].rearrange("(r p) e -> p r e", p=P),
             )
 
-        nc.vector.memset(scale_rows[:].bitcast(I32), 0)
+        nc.vector.memset(pool_scale_rows[:].bitcast(I32), 0)
+        nc.vector.memset(cand_s[:].bitcast(I32), 0)
         nc.vector.memset(vec_rows[:], 0.0)
-        nc.vector.memset(table_warm[:], 0.0)
-        nc.scalar.activation(out=table_warm[:, 1:2], in_=table_warm[:, 0:1], func=ACT.Relu)
-        load_users(nc.gpsimd, 0)
-        load_users(nc.gpsimd, 1)
+        zeros_w = sbuf("zeros_w", [P, N // 2], U32)
+        zeros_s = sbuf("zeros_s", [P, N // 2], U8)
+        nc.vector.quantize_mx(out=zeros_w[:].bitcast(FP8X4), scales=zeros_s[:], in_=vec_rows[:].bitcast(BF16))
+        nc.vector.memset(later_scales[:].bitcast(I32), 0)
+        nc.gpsimd.dma_start(out=vec_raw[0:4, :], in_=covered.rearrange("(g m) -> g m", g=4))
+        nc.gpsimd.dma_start(out=vec_raw[32:36, :], in_=prior.rearrange("(g m) -> g m", g=4))
         make_identity(nc, ident[:])
-        nc.sync.dma_start(out=vec_raw[0:4, :], in_=covered.rearrange("(g m) -> g m", g=4))
-        nc.sync.dma_start(out=vec_raw[32:36, :], in_=prior.rearrange("(g m) -> g m", g=4))
-        load_words(cand_w[0], cand_words32, 0)
+        nc.scalar.activation(out=table_warm[:], in_=vec_rows[:, 0:2], func=ACT.Relu)
         load_words(pool_raw[0], pool_words32, 0)
-        for r in range(4):
-            nc.sync.dma_start(out=pool_scale_raw[r:P:32].bitcast(I32), in_=pool_scales32[r])
-        for r in range(4):
-            nc.sync.dma_start(out=cand_s[r:P:32].bitcast(I32), in_=cand_scales32[r])
-        load_traits(0)
-        load_words(pool_raw[1], pool_words32, 1)
-        load_words(cand_w[1], cand_words32, 1)
+        load_words(cand_w[0], cand_words32, 0)
+        nc.sync.dma_start(out=pool_scale_rows[0:P:32].bitcast(I32), in_=pool_scales32[0][:, :, : N // 4])
+        nc.sync.dma_start(out=pool_scale_rows[1:P:32].bitcast(I32), in_=pool_scales32[1][:, :, : N // 4])
+        nc.sync.dma_start(out=pool_scale_rows[2:P:32].bitcast(I32), in_=pool_scales32[2][:, :, : N // 4])
+        nc.sync.dma_start(out=pool_scale_rows[3:P:32].bitcast(I32), in_=pool_scales32[3][:, :, : N // 4])
+        nc.sync.dma_start(out=cand_s[0:P:32].bitcast(I32), in_=cand_scales32[0])
+        load_users(nc.sync, 0)
+        nc.sync.dma_start(out=cand_s[1:P:32].bitcast(I32), in_=cand_scales32[1])
+        nc.sync.dma_start(out=cand_s[2:P:32].bitcast(I32), in_=cand_scales32[2])
+        nc.sync.dma_start(out=cand_s[3:P:32].bitcast(I32), in_=cand_scales32[3])
+        load_traits(0, 0)
         load_words(pool_raw[2], pool_words32, 2)
-        load_traits(1)
+        nc.sync.dma_start(out=later_scales[0:P:32].bitcast(I32), in_=pool_scales32[0][:, :, N // 4 :])
+        load_words(cand_w[1], cand_words32, 1)
+        nc.sync.dma_start(out=later_scales[3:P:32].bitcast(I32), in_=pool_scales32[3][:, :, N // 4 :])
+        nc.sync.dma_start(out=later_scales[2:P:32].bitcast(I32), in_=pool_scales32[2][:, :, N // 4 :])
+        nc.sync.dma_start(out=later_scales[1:P:32].bitcast(I32), in_=pool_scales32[1][:, :, N // 4 :])
         load_words(pool_raw[3], pool_words32, 3)
-        load_traits(2)
-        load_traits(3)
+        load_traits(0, 1)
+        load_words(pool_raw[1], pool_words32, 1)
+        load_traits(2, 1)
+        load_traits(2, 0)
+        load_traits(1, 0)
+        load_traits(1, 1)
+        load_users(nc.sync, 1)
+        load_traits(3, 1)
+        load_traits(3, 0)
 
+        def warm_up(count):
+            b, bank = take_bank()
+            for i in range(count):
+                nc.tensor.matmul_mx(
+                    out=bank[:, : N // 2], lhsT=zeros_w[:, :P].bitcast(FP8X4), lhsT_scale=zeros_s[:, :P],
+                    rhs=zeros_w[:].bitcast(FP8X4), rhs_scale=zeros_s[:], start=True, stop=True,
+                )
+            free_banks.append(b)
+
+        def group_traits_pass(k, t, engine):
+            if 0 not in traits_grouped:
+                traits_grouped[0] = sbuf("traits_grouped0", [P, 4, 2 * N], BF16, tag="traits_grouped", bufs=2)
+            copy(
+                engine,
+                traits_grouped[0][:, t, k * N : (k + 1) * N].rearrange("p (b h i j) -> p b h j i", h=2, i=4, j=4),
+                traits_raw[0][:, :, k, :].rearrange("p j (b t h i) -> p t b h j i", t=4, h=2, i=4)[:, t],
+            )
 
         def permute_pool(g):
             nc.vector.tensor_copy(
@@ -229,7 +301,7 @@ def tile_facility_location_gain_s12_kernel(
             )
             nc.vector.tensor_copy(
                 out=pool_s[g][:].bitcast(I32).rearrange("p k (t b w) -> p k t b w", t=4, w=2),
-                in_=pool_scale_raw[:, :, g * N : (g + 1) * N].bitcast(I32).rearrange("p k (b t w) -> p k t b w", t=4, w=2),
+                in_=pool_scale_raw[g].bitcast(I32).rearrange("p k (b t w) -> p k t b w", t=4, w=2),
             )
 
         def make_bias():
@@ -287,7 +359,7 @@ def tile_facility_location_gain_s12_kernel(
             )
 
         def first_stage(g, h):
-            rows[g, h] = sbuf("rows%d_%d" % (g, h), [P, 4, N], BF16, tag="rows", bufs=8)
+            rows[g, h] = sbuf("rows%d_%d" % (g, h), [P, 4, N], BF16, tag="rows", bufs=9)
             for t in range(4):
                 b, bank = take_bank()
                 for k in range(2):
@@ -311,12 +383,13 @@ def tile_facility_location_gain_s12_kernel(
                 free_banks.append(b)
 
         def interleave(g, h, half, engine):
+            c0, c1 = COLUMN_PIECES[h][half]
             if (g, h) not in grouped:
-                grouped[g, h] = sbuf("grouped%d_%d" % (g, h), [P, 4 * N], BF16, tag="grouped", bufs=4)
+                grouped[g, h] = sbuf("grouped%d_%d" % (g, h), [P, 4 * N], BF16, tag="grouped", bufs=5)
             copy(
                 engine,
-                grouped[g, h][:, half * 2 * N : (half + 1) * 2 * N].rearrange("p (c i t) -> p c t i", i=4, t=4),
-                rows[g, h][:, :, half * 256 : (half + 1) * 256].rearrange("p t (c i) -> p c t i", i=4),
+                grouped[g, h][:, 4 * c0 : 4 * c1].rearrange("p (c i t) -> p c t i", i=4, t=4),
+                rows[g, h][:, :, c0:c1].rearrange("p t (c i) -> p c t i", i=4),
             )
 
         def quantize_result(g, h):
@@ -336,12 +409,49 @@ def tile_facility_location_gain_s12_kernel(
 
         def finish(h, r, engine):
             b, bank = acc[h, r]
-            result = sbuf("result%d_%d" % (h, r), [P, N], F32, tag="result", bufs=8)
+            result = sbuf("result%d_%d" % (h, r), [P, N], F32, tag="result", bufs=4)
             copy(engine, result[:], bank[:])
             free_banks.append(b)
             nc.sync.dma_start(out=out[r * P : (r + 1) * P, h * N : (h + 1) * N], in_=result[:])
 
+        def quantize_half(g, half):
+            c0, c1 = COLUMN_PIECES[1][half]
+            cols = slice(c0, c1)
+            nc.vector.quantize_mx(
+                out=words[g, 1][:, cols].bitcast(FP8X4), scales=scales[g, 1][:, cols],
+                in_=grouped[g, 1][:, 4 * c0 : 4 * c1],
+            )
+
+        def second_stage_half(g, half, first, last):
+            c0, c1 = COLUMN_PIECES[1][half]
+            ncols = slice(c0, c1)
+            for r in range(4):
+                if first:
+                    acc[1 + half, r] = take_bank()
+                cols = slice(r * P, (r + 1) * P)
+                nc.tensor.matmul_mx(
+                    out=acc[1 + half, r][1][:, : c1 - c0],
+                    lhsT=words[g, INTEREST][:, cols].bitcast(FP8X4), lhsT_scale=scales[g, INTEREST][:, cols],
+                    rhs=words[g, 1][:, ncols].bitcast(FP8X4), rhs_scale=scales[g, 1][:, ncols],
+                    start=first, stop=last,
+                )
+
+        def finish_half(half, r, engine):
+            b, bank = acc[1 + half, r]
+            c0, c1 = COLUMN_PIECES[1][half]
+            per_store = TILES_PER_STORE[half]
+            r0 = r - r % per_store
+            if r == r0:
+                results[half, r0] = sbuf("result_half%d_%d" % (half, r0), [P, per_store, c1 - c0], F32)
+            copy(engine, results[half, r0][:, r - r0, :], bank[:, : c1 - c0])
+            free_banks.append(b)
+            if r == r0 + per_store - 1:
+                dst = out[r0 * P : (r + 1) * P, N + c0 : N + c1]
+                nc.sync.dma_start(out=dst.rearrange("(r p) c -> p r c", p=P), in_=results[half, r0][:])
+
         steps = {
+            "W": warm_up, "TK": group_traits_pass,
+            "QH": quantize_half, "OH": second_stage_half, "FH": finish_half,
             "P": permute_pool, "B": make_bias, "T": transpose_users, "UQ": quantize_users,
             "TI": group_traits, "TQ": quantize_traits, "S": first_stage, "IL": interleave,
             "Q": quantize_result, "O": second_stage, "F": finish,

@@ -17,146 +17,56 @@ ACT = mybir.ActivationFunctionType
 ALU = mybir.AluOpType
 
 P = 128
+PACK = 4
 N = 512
+PASSES = 2
 GROUPS = M // N
-INTEREST = 2
+USER_TILES = U // P
+BANKS = 8
 
-COLUMN_PIECES = {0: [(0, 256), (256, 512)], 1: [(0, 256), (256, 384), (384, 512)], 2: [(0, 256), (256, 512)]}
+GAIN_LO, GAIN_HI, INTEREST = 0, 1, 2
+WHOLE = 2
+COLUMNS = [slice(0, N // 2), slice(N // 2, N), slice(0, N)]
+VECTOR, SCALAR = 0, 1
 
-TILES_PER_STORE = [1, 4, 2]
+ROWS_BUFS = 9
+GROUPED_BUFS = 5
+TRAITS_BUFS = 2
 
-SCHEDULE = [
-    ("W", 9,),
-    ("B",),
-    ("W", 4,),
-    ("P", 0,),
-    ("TK", 0, 1, "V",),
-    ("T", 0, "A",),
-    ("TK", 0, 0, "V",),
-    ("TK", 0, 3, "V",),
-    ("TK", 0, 2, "V",),
-    ("UQ", 0,),
-    ("S", 0, 0,),
-    ("P", 2,),
-    ("IL", 0, 0, 1, "V",),
-    ("S", 0, 1,),
-    ("IL", 0, 0, 0, "V",),
-    ("P", 3,),
-    ("TK", 1, 0, "V",),
-    ("P", 1,),
-    ("IL", 0, 1, 0, "V",),
-    ("TK", 1, 3, "V",),
-    ("TK", 1, 2, "V",),
-    ("TK", 1, 1, "V",),
-    ("TQ", 0, 1,),
-    ("TI", 2, 1, "V",),
-    ("TI", 2, 2, "V",),
-    ("TQ", 0, 0,),
-    ("S", 2, 0,),
-    ("TI", 2, 0, "V",),
-    ("TI", 2, 3, "V",),
-    ("S", 3, 0,),
-    ("TQ", 2, 0,),
-    ("TI", 1, 3, "V",),
-    ("TQ", 2, 1,),
-    ("S", 1, 0,),
-    ("Q", 0, 0,),
-    ("TI", 1, 1, "V",),
-    ("TI", 1, 0, "V",),
-    ("IL", 1, 0, 0, "V",),
-    ("IL", 3, 0, 1, "A",),
-    ("T", 1, "A",),
-    ("IL", 3, 0, 0, "V",),
-    ("S", 3, 1,),
-    ("TI", 3, 2, "V",),
-    ("TI", 3, 1, "V",),
-    ("S", 1, 1,),
-    ("UQ", 1,),
-    ("S", 0, 2,),
-    ("TI", 3, 0, "V",),
-    ("IL", 2, 0, 0, "V",),
-    ("TI", 1, 2, "V",),
-    ("TQ", 1, 0,),
-    ("IL", 2, 0, 1, "V",),
-    ("TQ", 3, 0,),
-    ("TQ", 1, 1,),
-    ("S", 2, 2,),
-    ("IL", 0, 2, 1, "V",),
-    ("IL", 0, 1, 1, "V",),
-    ("S", 1, 2,),
-    ("IL", 0, 2, 0, "V",),
-    ("TI", 3, 3, "V",),
-    ("Q", 0, 2,),
-    ("IL", 1, 0, 1, "V",),
-    ("TQ", 3, 1,),
-    ("Q", 1, 0,),
-    ("QH", 0, 0,),
-    ("IL", 1, 2, 0, "V",),
-    ("Q", 2, 0,),
-    ("IL", 1, 2, 1, "V",),
-    ("S", 3, 2,),
-    ("IL", 2, 2, 1, "V",),
-    ("IL", 2, 2, 0, "A",),
-    ("IL", 3, 2, 0, "V",),
-    ("Q", 1, 2,),
-    ("IL", 3, 2, 1, "A",),
-    ("O", 0, 0, True, False,),
-    ("S", 2, 1,),
-    ("Q", 2, 2,),
-    ("IL", 0, 1, 2, "V",),
-    ("Q", 3, 0,),
-    ("O", 1, 0, False, False,),
-    ("O", 2, 0, False, False,),
-    ("IL", 3, 1, 0, "A",),
-    ("Q", 3, 2,),
-    ("QH", 0, 1,),
-    ("IL", 1, 1, 1, "V",),
-    ("O", 3, 0, False, True,),
-    ("IL", 1, 1, 0, "V",),
-    ("OH", 0, 0, True, False,),
-    ("F", 0, 0, "A",),
-    ("IL", 2, 1, 0, "V",),
-    ("QH", 1, 0,),
-    ("OH", 1, 0, False, False,),
-    ("QH", 2, 0,),
-    ("OH", 2, 0, False, False,),
-    ("F", 0, 1, "A",),
-    ("QH", 3, 0,),
-    ("IL", 3, 1, 1, "V",),
-    ("QH", 1, 1,),
-    ("IL", 2, 1, 1, "V",),
-    ("IL", 2, 1, 2, "V",),
-    ("F", 0, 2, "A",),
-    ("OH", 3, 0, False, True,),
-    ("QH", 3, 1,),
-    ("FH", 0, 0, "A",),
-    ("OH", 0, 1, True, False,),
-    ("F", 0, 3, "A",),
-    ("OH", 1, 1, False, False,),
-    ("IL", 1, 1, 2, "V",),
-    ("QH", 2, 1,),
-    ("OH", 2, 1, False, False,),
-    ("FH", 0, 1, "V",),
-    ("FH", 0, 2, "A",),
-    ("QH", 0, 2,),
-    ("OH", 3, 1, False, True,),
-    ("FH", 0, 3, "A",),
-    ("IL", 3, 1, 2, "V",),
-    ("OH", 0, 2, True, False,),
-    ("QH", 1, 2,),
-    ("FH", 1, 0, "V",),
-    ("FH", 1, 1, "A",),
-    ("QH", 2, 2,),
-    ("OH", 1, 2, False, False,),
-    ("QH", 3, 2,),
-    ("OH", 2, 2, False, False,),
-    ("FH", 1, 2, "A",),
-    ("FH", 1, 3, "V",),
-    ("OH", 3, 2, False, True,),
-    ("FH", 2, 0, "A",),
-    ("FH", 2, 1, "V",),
-    ("FH", 2, 2, "A",),
-    ("FH", 2, 3, "V",),
+STEPS = [
+    ("warm", 7), ("bias",), ("warm", 5), ("pool", 0), ("first", 0, GAIN_LO), ("pool", 1), ("pool", 2),
+    ("pool", 3), ("first", 1, GAIN_LO), ("group", 0, GAIN_LO, 0, VECTOR), ("group", 0, GAIN_LO, 1, VECTOR),
+    ("traits", 0, 0, 2, VECTOR), ("traits", 0, 0, 3, VECTOR), ("traits", 0, 0, 0, VECTOR),
+    ("group", 1, GAIN_LO, 0, VECTOR), ("traits", 0, 0, 1, VECTOR), ("first", 3, GAIN_LO), ("first", 2, GAIN_LO),
+    ("traits", 0, 1, 1, VECTOR), ("traits_q", 0, 0, 1), ("traits", 0, 1, 3, VECTOR),
+    ("traits", 0, 1, 2, VECTOR), ("traits", 0, 1, 0, VECTOR), ("first", 0, GAIN_HI),
+    ("group", 3, GAIN_LO, 1, VECTOR), ("group", 3, GAIN_LO, 0, VECTOR), ("traits_q", 0, 1, 0),
+    ("traits_q", 0, 1, 1), ("group", 1, GAIN_LO, 1, VECTOR), ("users", 1, SCALAR), ("first", 2, GAIN_HI),
+    ("users", 0, SCALAR), ("group", 2, GAIN_LO, 0, VECTOR), ("traits", 1, 0, 2, VECTOR), ("traits_q", 0, 0, 0),
+    ("result_q", 3, GAIN_LO, WHOLE), ("users_q", 1), ("traits", 1, 0, 0, VECTOR), ("first", 1, GAIN_HI),
+    ("traits", 1, 1, 1, VECTOR), ("users_q", 0), ("traits", 1, 1, 0, VECTOR), ("first", 0, INTEREST),
+    ("traits", 1, 0, 3, VECTOR), ("traits", 1, 1, 3, VECTOR), ("first", 1, INTEREST), ("traits_q", 1, 0, 1),
+    ("traits", 1, 0, 1, VECTOR), ("traits_q", 1, 1, 0), ("traits", 1, 1, 2, VECTOR), ("traits_q", 1, 0, 0),
+    ("group", 0, INTEREST, 1, VECTOR), ("traits_q", 1, 1, 1), ("group", 0, INTEREST, 0, VECTOR),
+    ("first", 2, INTEREST), ("result_q", 1, GAIN_LO, WHOLE), ("group", 1, INTEREST, 1, VECTOR),
+    ("first", 3, INTEREST), ("group", 2, GAIN_LO, 1, SCALAR), ("group", 1, INTEREST, 0, VECTOR),
+    ("result_q", 0, INTEREST, WHOLE), ("group", 0, GAIN_HI, 0, VECTOR), ("group", 2, INTEREST, 0, VECTOR),
+    ("group", 2, INTEREST, 1, VECTOR), ("result_q", 0, GAIN_LO, WHOLE), ("group", 3, INTEREST, 0, SCALAR),
+    ("result_q", 0, GAIN_HI, 0), ("first", 3, GAIN_HI), ("second", 0, GAIN_LO, WHOLE),
+    ("result_q", 1, INTEREST, WHOLE), ("group", 3, INTEREST, 1, VECTOR), ("result_q", 2, INTEREST, WHOLE),
+    ("result_q", 2, GAIN_LO, WHOLE), ("result_q", 3, INTEREST, WHOLE), ("second", 1, GAIN_LO, WHOLE),
+    ("second", 2, GAIN_LO, WHOLE), ("group", 2, GAIN_HI, 0, SCALAR), ("group", 1, GAIN_HI, 0, VECTOR),
+    ("group", 1, GAIN_HI, 1, VECTOR), ("group", 3, GAIN_HI, 0, VECTOR), ("result_q", 1, GAIN_HI, 0),
+    ("result_q", 2, GAIN_HI, 0), ("second", 3, GAIN_LO, WHOLE), ("store", GAIN_LO, WHOLE, 0, SCALAR),
+    ("second", 0, GAIN_HI, 0), ("second", 1, GAIN_HI, 0), ("group", 0, GAIN_HI, 1, VECTOR),
+    ("store", GAIN_LO, WHOLE, 1, SCALAR), ("result_q", 3, GAIN_HI, 0), ("second", 2, GAIN_HI, 0),
+    ("result_q", 0, GAIN_HI, 1), ("group", 2, GAIN_HI, 1, VECTOR), ("second", 3, GAIN_HI, 0),
+    ("store", GAIN_LO, WHOLE, 2, SCALAR), ("store", GAIN_LO, WHOLE, 3, SCALAR), ("second", 0, GAIN_HI, 1),
+    ("result_q", 1, GAIN_HI, 1), ("second", 1, GAIN_HI, 1), ("store", GAIN_HI, 0, 0, VECTOR),
+    ("result_q", 2, GAIN_HI, 1), ("group", 3, GAIN_HI, 1, SCALAR), ("store", GAIN_HI, 0, 1, SCALAR),
+    ("second", 2, GAIN_HI, 1), ("store", GAIN_HI, 0, 2, SCALAR), ("result_q", 3, GAIN_HI, 1),
+    ("store", GAIN_HI, 0, 3, VECTOR), ("second", 3, GAIN_HI, 1), ("store", GAIN_HI, 1, 0, SCALAR),
+    ("store", GAIN_HI, 1, 1, VECTOR), ("store", GAIN_HI, 1, 2, SCALAR), ("store", GAIN_HI, 1, 3, VECTOR),
 ]
 
 
@@ -165,296 +75,247 @@ def tile_facility_location_gain_s12_kernel(
 ):
     nc = tc.nc
     with ExitStack() as ctx:
-        keep = ctx.enter_context(tc.tile_pool(name="keep", bufs=1))
+        sb = ctx.enter_context(tc.tile_pool(name="sb", bufs=1))
         psum = ctx.enter_context(tc.psum_pool(name="psum", bufs=1))
         ctx.enter_context(tc.manual_schedule())
 
         def sbuf(name, shape, dtype, tag=None, bufs=1):
-            return keep.tile(shape, dtype, name=name, tag=tag or name, bufs=bufs, align_bytes=64)
+            return sb.tile(shape, dtype, name=name, tag=tag or name, bufs=bufs, align_bytes=64)
 
-        def copy(engine, out, in_):
-            if engine == "V":
-                nc.vector.tensor_copy(out=out, in_=in_)
+        def copy(engine, dst, src):
+            if engine == VECTOR:
+                nc.vector.tensor_copy(out=dst, in_=src)
             else:
-                nc.scalar.copy(out=out, in_=in_)
+                nc.scalar.copy(out=dst, in_=src)
 
-        free_banks = list(range(8))
-        bank_uses = []
+        def quantize(codes, scales, values):
+            nc.vector.quantize_mx(out=codes.bitcast(FP8X4), scales=scales, in_=values)
+
+        free_banks = list(range(BANKS))
+        taken = []
 
         def take_bank():
             b = free_banks.pop(0)
-            bank_uses.append(b)
-            return b, psum.tile([P, N], F32, name="acc%d" % len(bank_uses), tag="bank%d" % b)
+            taken.append(b)
+            return b, psum.tile([P, N], F32, name="acc%d" % len(taken), tag="bank%d" % b)
 
-        pool_scale_rows = sbuf("pool_scale_rows", [P, 2, N], U8)
-        later_scales = sbuf("later_scales", [P, 2, M - N], U8)
-        pool_scale_raw = [pool_scale_rows[:]] + [later_scales[:, :, g * N : (g + 1) * N] for g in range(GROUPS - 1)]
-        cand_s = sbuf("cand_s", [P, 2, C], U8)
-        vec_raw = sbuf("vec_raw", [P, N], BF16)
-        vec_rows = sbuf("vec_rows", [P, N], F32)
-        bias = sbuf("bias", [P, 32], F32)
-        ident = sbuf("ident", [P, P], F32)
-        table_warm = sbuf("table_warm", [P, 2], F32)
-        cand_w = [sbuf("cand_w%d" % h, [P, 2, 2 * N], U8) for h in range(2)]
-        pool_raw = [sbuf("pool_raw%d" % g, [P, 2, 2 * N], U8) for g in range(GROUPS)]
-        pool_w = [sbuf("pool_w%d" % g, [P, 2, 2 * N], U8) for g in range(GROUPS)]
-        pool_s = [sbuf("pool_s%d" % g, [P, 2, N], U8) for g in range(GROUPS)]
-        users_raw = [sbuf("users_raw%d" % k, [P, 4 * N], BF16) for k in range(2)]
-        users_grouped = [sbuf("users_grouped%d" % k, [P, 4 * N], BF16) for k in range(2)]
-        users_w = [sbuf("users_w%d" % k, [P, N], U32) for k in range(2)]
-        users_s = [sbuf("users_s%d" % k, [P, N], U8) for k in range(2)]
-        traits_raw = [sbuf("traits_raw%d" % g, [P, 4, 2, N], BF16) for g in range(GROUPS)]
-        traits_w = [sbuf("traits_w%d" % g, [P, 2 * N], U32) for g in range(GROUPS)]
-        traits_s = [sbuf("traits_s%d" % g, [P, 2 * N], U8) for g in range(GROUPS)]
-        traits_grouped = {}
-        rows = {}
-        grouped = {}
-        words = {}
-        scales = {}
+        cand_codes = [sbuf("cand_codes%d" % h, [P, PASSES, 2 * N], U8) for h in range(2)]
+        cand_scales_sb = sbuf("cand_scales_sb", [P, PASSES, C], U8)
+        pool_raw_first = sbuf("pool_raw_first", [P, PASSES, 2 * N], U8)
+        pool_raw_rest = sbuf("pool_raw_rest", [P, PASSES, 2 * (M - N)], U8)
+        pool_raw = [pool_raw_first[:]] + [pool_raw_rest[:, :, 2 * N * j : 2 * N * (j + 1)] for j in range(GROUPS - 1)]
+        pool_scales_raw = sbuf("pool_scales_raw", [P, PASSES, M], U8)
+        pool_codes = [sbuf("pool_codes%d" % g, [P, PASSES, 2 * N], U8) for g in range(GROUPS)]
+        pool_scales_sb = [sbuf("pool_scales_sb%d" % g, [P, PASSES, N], U8) for g in range(GROUPS)]
+        vector_rows = sbuf("vector_rows", [P, N], BF16)
+        vector_slots = sbuf("vector_slots", [P, N], F32)
+        bias_columns = sbuf("bias_columns", [P, PACK, 2, GROUPS], F32)
+        identity = sbuf("identity", [P, P], F32)
+        table_out = sbuf("table_out", [P, 2], F32)
+        zero_codes = sbuf("zero_codes", [P, N // 2], U32)
+        zero_scales = sbuf("zero_scales", [P, N // 2], U8)
+        users_raw = sbuf("users_raw", [P, USER_TILES * E], BF16)
+        users_grouped = [sbuf("users_grouped%d" % k, [P, PACK * U], BF16) for k in range(PASSES)]
+        users_codes = [sbuf("users_codes%d" % k, [P, U], U32) for k in range(PASSES)]
+        users_scales = [sbuf("users_scales%d" % k, [P, U], U8) for k in range(PASSES)]
+        traits_raw, traits_codes, traits_scales = {}, {}, {}
+        for pair in range(GROUPS // 2):
+            for k in range(PASSES):
+                traits_raw[pair, k] = sbuf("traits_raw%d_%d" % (pair, k), [P, PACK, 2 * N], BF16)
+                traits_codes[pair, k] = sbuf("traits_codes%d_%d" % (pair, k), [P, PACK, 2 * P], U32)
+                traits_scales[pair, k] = sbuf("traits_scales%d_%d" % (pair, k), [P, PACK, 2 * P], U8)
+        result_codes, result_scales = {}, {}
         for g in range(GROUPS):
-            for h in range(3):
-                words[g, h] = sbuf("words%d_%d" % (g, h), [P, N], U32)
-                scales[g, h] = sbuf("scales%d_%d" % (g, h), [P, N], U8)
-        acc = {}
-        results = {}
+            for kind in (GAIN_LO, GAIN_HI, INTEREST):
+                result_codes[g, kind] = sbuf("result_codes%d_%d" % (g, kind), [P, N], U32)
+                result_scales[g, kind] = sbuf("result_scales%d_%d" % (g, kind), [P, N], U8)
+        traits_grouped, result_rows, result_grouped, out_banks, out_tiles = {}, {}, {}, {}, {}
 
-        pool_words32 = pool_words.bitcast(I32).rearrange("k p n -> p k n")
-        cand_words32 = cand_words.bitcast(I32).rearrange("k p n -> p k n")
-        pool_scales32 = pool_scales.bitcast(I32).rearrange("k (q r) n -> r q k n", r=4)
-        cand_scales32 = cand_scales.bitcast(I32).rearrange("k (q r) n -> r q k n", r=4)
+        def load_fp4_words(dst, words, first_column):
+            src = words.bitcast(I32).rearrange("k p n -> p k n")
+            width = dst.shape[2] // 4
+            nc.sync.dma_start(out=dst[:].bitcast(I32), in_=src[:, :, first_column // 2 : first_column // 2 + width])
 
-        def load_words(dst, src, j):
-            nc.sync.dma_start(out=dst[:].bitcast(I32), in_=src[:, :, j * 256 : (j + 1) * 256])
+        def load_scale_rows(dst, scales):
+            src = scales.bitcast(I32).rearrange("k (q r) n -> r q k n", r=4)
+            for r in range(4):
+                nc.sync.dma_start(out=dst[r:P:32].bitcast(I32), in_=src[r])
 
-        def load_traits(g, k):
-            src = traits[k * N : (k + 1) * N, g * N : (g + 1) * N]
-            nc.sync.dma_start(out=traits_raw[g][:, :, k, :], in_=src.rearrange("(p j) m -> p j m", j=4))
+        def load_traits(pair, k):
+            src = traits[k * N : (k + 1) * N, pair * 2 * N : (pair + 1) * 2 * N]
+            nc.sync.dma_start(out=traits_raw[pair, k][:], in_=src.rearrange("(p j) m -> p j m", j=PACK))
 
-        def load_users(queue, k):
-            queue.dma_start(
-                out=users_raw[k][:].rearrange("p (r e) -> p r e", r=4),
-                in_=users[:, k * N : (k + 1) * N].rearrange("(r p) e -> p r e", p=P),
-            )
+        nc.vector.memset(pool_scales_raw[:].bitcast(I32), 0)
+        nc.vector.memset(cand_scales_sb[:].bitcast(I32), 0)
+        nc.gpsimd.memset(vector_slots[:], 0.0)
+        make_identity(nc, identity[:])
+        quantize(zero_codes[:], zero_scales[:], vector_slots[:].bitcast(BF16))
+        nc.scalar.activation(out=table_out[:], in_=vector_slots[:, 0:2], func=ACT.Relu)
 
-        nc.vector.memset(pool_scale_rows[:].bitcast(I32), 0)
-        nc.vector.memset(cand_s[:].bitcast(I32), 0)
-        nc.vector.memset(vec_rows[:], 0.0)
-        zeros_w = sbuf("zeros_w", [P, N // 2], U32)
-        zeros_s = sbuf("zeros_s", [P, N // 2], U8)
-        nc.vector.quantize_mx(out=zeros_w[:].bitcast(FP8X4), scales=zeros_s[:], in_=vec_rows[:].bitcast(BF16))
-        nc.vector.memset(later_scales[:].bitcast(I32), 0)
-        nc.gpsimd.dma_start(out=vec_raw[0:4, :], in_=covered.rearrange("(g m) -> g m", g=4))
-        nc.gpsimd.dma_start(out=vec_raw[32:36, :], in_=prior.rearrange("(g m) -> g m", g=4))
-        make_identity(nc, ident[:])
-        nc.scalar.activation(out=table_warm[:], in_=vec_rows[:, 0:2], func=ACT.Relu)
-        load_words(pool_raw[0], pool_words32, 0)
-        load_words(cand_w[0], cand_words32, 0)
-        nc.sync.dma_start(out=pool_scale_rows[0:P:32].bitcast(I32), in_=pool_scales32[0][:, :, : N // 4])
-        nc.sync.dma_start(out=pool_scale_rows[1:P:32].bitcast(I32), in_=pool_scales32[1][:, :, : N // 4])
-        nc.sync.dma_start(out=pool_scale_rows[2:P:32].bitcast(I32), in_=pool_scales32[2][:, :, : N // 4])
-        nc.sync.dma_start(out=pool_scale_rows[3:P:32].bitcast(I32), in_=pool_scales32[3][:, :, : N // 4])
-        nc.sync.dma_start(out=cand_s[0:P:32].bitcast(I32), in_=cand_scales32[0])
-        load_users(nc.sync, 0)
-        nc.sync.dma_start(out=cand_s[1:P:32].bitcast(I32), in_=cand_scales32[1])
-        nc.sync.dma_start(out=cand_s[2:P:32].bitcast(I32), in_=cand_scales32[2])
-        nc.sync.dma_start(out=cand_s[3:P:32].bitcast(I32), in_=cand_scales32[3])
+        nc.sync.dma_start(out=vector_rows[0:4, :], in_=covered.rearrange("(g m) -> g m", g=GROUPS))
+        nc.sync.dma_start(out=vector_rows[32:36, :], in_=prior.rearrange("(g m) -> g m", g=GROUPS))
+        load_fp4_words(cand_codes[0], cand_words, 0)
+        load_fp4_words(pool_raw_first, pool_words, 0)
+        load_scale_rows(pool_scales_raw, pool_scales)
+        load_scale_rows(cand_scales_sb, cand_scales)
+        load_fp4_words(pool_raw_rest, pool_words, N)
         load_traits(0, 0)
-        load_words(pool_raw[2], pool_words32, 2)
-        nc.sync.dma_start(out=later_scales[0:P:32].bitcast(I32), in_=pool_scales32[0][:, :, N // 4 :])
-        load_words(cand_w[1], cand_words32, 1)
-        nc.sync.dma_start(out=later_scales[3:P:32].bitcast(I32), in_=pool_scales32[3][:, :, N // 4 :])
-        nc.sync.dma_start(out=later_scales[2:P:32].bitcast(I32), in_=pool_scales32[2][:, :, N // 4 :])
-        nc.sync.dma_start(out=later_scales[1:P:32].bitcast(I32), in_=pool_scales32[1][:, :, N // 4 :])
-        load_words(pool_raw[3], pool_words32, 3)
         load_traits(0, 1)
-        load_words(pool_raw[1], pool_words32, 1)
-        load_traits(2, 1)
-        load_traits(2, 0)
+        load_fp4_words(cand_codes[1], cand_words, N)
+        nc.sync.dma_start(out=users_raw[:], in_=users.rearrange("(p r) e -> p (r e)", r=USER_TILES))
         load_traits(1, 0)
         load_traits(1, 1)
-        load_users(nc.sync, 1)
-        load_traits(3, 1)
-        load_traits(3, 0)
 
-        def warm_up(count):
+        def warm(count):
             b, bank = take_bank()
             for i in range(count):
                 nc.tensor.matmul_mx(
-                    out=bank[:, : N // 2], lhsT=zeros_w[:, :P].bitcast(FP8X4), lhsT_scale=zeros_s[:, :P],
-                    rhs=zeros_w[:].bitcast(FP8X4), rhs_scale=zeros_s[:], start=True, stop=True,
+                    out=bank[:, : N // 2],
+                    lhsT=zero_codes[:, :P].bitcast(FP8X4), lhsT_scale=zero_scales[:, :P],
+                    rhs=zero_codes[:].bitcast(FP8X4), rhs_scale=zero_scales[:],
+                    start=True, stop=True,
                 )
             free_banks.append(b)
 
-        def group_traits_pass(k, t, engine):
-            if 0 not in traits_grouped:
-                traits_grouped[0] = sbuf("traits_grouped0", [P, 4, 2 * N], BF16, tag="traits_grouped", bufs=2)
-            copy(
-                engine,
-                traits_grouped[0][:, t, k * N : (k + 1) * N].rearrange("p (b h i j) -> p b h j i", h=2, i=4, j=4),
-                traits_raw[0][:, :, k, :].rearrange("p j (b t h i) -> p t b h j i", t=4, h=2, i=4)[:, t],
-            )
-
-        def permute_pool(g):
-            nc.vector.tensor_copy(
-                out=pool_w[g][:].bitcast(I32).rearrange("p k (t b w) -> p k t b w", t=4, w=4),
-                in_=pool_raw[g][:].bitcast(I32).rearrange("p k (b t w) -> p k t b w", t=4, w=4),
-            )
-            nc.vector.tensor_copy(
-                out=pool_s[g][:].bitcast(I32).rearrange("p k (t b w) -> p k t b w", t=4, w=2),
-                in_=pool_scale_raw[g].bitcast(I32).rearrange("p k (b t w) -> p k t b w", t=4, w=2),
-            )
-
-        def make_bias():
-            nc.vector.tensor_scalar(
-                out=vec_rows[0:4, :].rearrange("g (t b i) -> g t b i", t=4, i=8),
-                in0=vec_raw[0:4, :].rearrange("g (b t i) -> g t b i", t=4, i=8),
-                scalar1=-1.0, scalar2=None, op0=ALU.mult,
-            )
-            nc.vector.tensor_copy(
-                out=vec_rows[32:36, :].rearrange("g (t b i) -> g t b i", t=4, i=8),
-                in_=vec_raw[32:36, :].rearrange("g (b t i) -> g t b i", t=4, i=8),
-            )
+        def bias():
+            by_slot = vector_slots[:].rearrange("g (t b i) -> g t b i", t=PACK, i=8)
+            by_item = vector_rows[:].rearrange("g (b t i) -> g t b i", t=PACK, i=8)
+            nc.vector.tensor_scalar(out=by_slot[0:4], in0=by_item[0:4], scalar1=-1.0, scalar2=None, op0=ALU.mult)
+            nc.vector.tensor_copy(out=by_slot[32:36], in_=by_item[32:36])
             b, bank = take_bank()
-            for t in range(4):
-                nc.tensor.transpose(bank[:, t * P : (t + 1) * P], vec_rows[:, t * P : (t + 1) * P], ident[:])
-            nc.vector.tensor_copy(
-                out=bias[:].rearrange("p (t v g) -> p t v g", t=4, v=2),
-                in_=bank[:].rearrange("p (t v g) -> p t v g", t=4, g=32)[:, :, 0:2, 0:4],
-            )
+            for t in range(PACK):
+                cols = slice(t * P, (t + 1) * P)
+                nc.tensor.transpose(bank[:, cols], vector_slots[:, cols], identity[:])
+            src = bank[:].rearrange("p (t v g) -> p t v g", t=PACK, g=32)
+            nc.vector.tensor_copy(out=bias_columns[:], in_=src[:, :, 0:2, 0:GROUPS])
             free_banks.append(b)
 
-        def transpose_users(k, engine):
-            pairs = users_raw[k][:].bitcast(F32)
-            dst = users_grouped[k][:].bitcast(F32).rearrange("p (r x u) -> p r x u", r=4, u=2)
-            for q in range(2):
+        def pool(g):
+            for dst, src, w in (
+                (pool_codes[g][:], pool_raw[g], 4),
+                (pool_scales_sb[g][:], pool_scales_raw[:, :, g * N : (g + 1) * N], 2),
+            ):
+                nc.vector.tensor_copy(
+                    out=dst.bitcast(I32).rearrange("p k (t b w) -> p k t b w", t=PACK, w=w),
+                    in_=src.bitcast(I32).rearrange("p k (b t w) -> p k t b w", t=PACK, w=w),
+                )
+
+        def users_step(k, engine):
+            pairs = users_raw[:].bitcast(F32)
+            dst = users_grouped[k][:].bitcast(F32).rearrange("p (r x u) -> p r x u", r=USER_TILES, u=2)
+            for r0 in range(0, USER_TILES, 2):
                 b, bank = take_bank()
-                for rr in range(2):
-                    r = 2 * q + rr
+                for r in (r0, r0 + 1):
+                    w0 = (r * E + k * N) // 2
                     for u in range(2):
-                        col = (2 * rr + u) * P
-                        nc.tensor.transpose(
-                            bank[:, col : col + P], pairs[:, 256 * r + u : 256 * (r + 1) : 2], ident[:]
-                        )
-                copy(engine, dst[:, 2 * q : 2 * q + 2], bank[:].rearrange("p (r u x) -> p r x u", r=2, u=2))
+                        col = (2 * (r - r0) + u) * P
+                        nc.tensor.transpose(bank[:, col : col + P], pairs[:, w0 + u : w0 + N // 2 : 2], identity[:])
+                copy(engine, dst[:, r0 : r0 + 2], bank[:].rearrange("p (r u x) -> p r x u", r=2, u=2))
                 free_banks.append(b)
 
-        def quantize_users(k):
-            nc.vector.quantize_mx(out=users_w[k][:].bitcast(FP8X4), scales=users_s[k][:], in_=users_grouped[k][:])
+        def users_q(k):
+            quantize(users_codes[k][:], users_scales[k][:], users_grouped[k][:])
 
-        def group_traits(g, t, engine):
-            if g not in traits_grouped:
-                traits_grouped[g] = sbuf("traits_grouped%d" % g, [P, 4, 2 * N], BF16, tag="traits_grouped", bufs=2)
+        def traits_step(pair, k, t, engine):
+            if (pair, k) not in traits_grouped:
+                traits_grouped[pair, k] = sbuf(
+                    "traits_grouped%d_%d" % (pair, k), [P, PACK, 2 * N], BF16, tag="traits_grouped", bufs=TRAITS_BUFS
+                )
             copy(
                 engine,
-                traits_grouped[g][:, t, :].rearrange("p (b h i j) -> p b h j i", h=2, i=4, j=4),
-                traits_raw[g][:].rearrange("p j k (b t h i) -> p t (k b) h j i", t=4, h=2, i=4)[:, t],
+                traits_grouped[pair, k][:, t, :].rearrange("p (b h i j) -> p b h j i", h=2, i=4, j=PACK),
+                traits_raw[pair, k][:].rearrange("p j (b t h i) -> p t b h j i", t=PACK, h=2, i=4)[:, t],
             )
 
-        def quantize_traits(g, half):
-            cols = slice(half * N, (half + 1) * N)
-            nc.vector.quantize_mx(
-                out=traits_w[g][:, cols].bitcast(FP8X4),
-                scales=traits_s[g][:, cols],
-                in_=traits_grouped[g][:, 2 * half : 2 * half + 2, :].rearrange("p t x -> p (t x)"),
+        def traits_q(pair, k, half):
+            slots = slice(2 * half, 2 * half + 2)
+            quantize(
+                traits_codes[pair, k][:, slots, :].rearrange("p t c -> p (t c)"),
+                traits_scales[pair, k][:, slots, :].rearrange("p t c -> p (t c)"),
+                traits_grouped[pair, k][:, slots, :].rearrange("p t c -> p (t c)"),
             )
 
-        def first_stage(g, h):
-            rows[g, h] = sbuf("rows%d_%d" % (g, h), [P, 4, N], BF16, tag="rows", bufs=9)
-            for t in range(4):
+        def first(g, kind):
+            result_rows[g, kind] = sbuf("result_rows%d_%d" % (g, kind), [P, PACK, N], BF16, tag="result_rows", bufs=ROWS_BUFS)
+            for t in range(PACK):
                 b, bank = take_bank()
-                for k in range(2):
-                    if h == INTEREST:
-                        cols = slice((2 * t + k) * P, (2 * t + k + 1) * P)
-                        lhsT, lhsT_scale = traits_w[g][:, cols].bitcast(FP8X4), traits_s[g][:, cols]
-                        rhs, rhs_scale = users_w[k][:].bitcast(FP8X4), users_s[k][:]
+                for k in range(PASSES):
+                    if kind == INTEREST:
+                        cols = slice((g % 2) * P, (g % 2 + 1) * P)
+                        lhsT = traits_codes[g // 2, k][:, t, cols].bitcast(FP8X4)
+                        lhsT_scale = traits_scales[g // 2, k][:, t, cols]
+                        rhs, rhs_scale = users_codes[k][:].bitcast(FP8X4), users_scales[k][:]
                     else:
-                        lhsT = pool_w[g][:, k, 2 * t * P : 2 * (t + 1) * P].bitcast(FP4X4)
-                        lhsT_scale = pool_s[g][:, k, t * P : (t + 1) * P]
-                        rhs, rhs_scale = cand_w[h][:, k, :].bitcast(FP4X4), cand_s[:, k, h * N : (h + 1) * N]
+                        lhsT = pool_codes[g][:, k, 2 * t * P : 2 * (t + 1) * P].bitcast(FP4X4)
+                        lhsT_scale = pool_scales_sb[g][:, k, t * P : (t + 1) * P]
+                        rhs = cand_codes[kind][:, k, :].bitcast(FP4X4)
+                        rhs_scale = cand_scales_sb[:, k, kind * N : (kind + 1) * N]
                     nc.tensor.matmul_mx(
                         out=bank[:], lhsT=lhsT, lhsT_scale=lhsT_scale, rhs=rhs, rhs_scale=rhs_scale,
-                        start=(k == 0), stop=(k == 1),
+                        start=(k == 0), stop=(k == PASSES - 1),
                     )
-                col = 8 * t + (4 if h == INTEREST else 0) + g
                 nc.scalar.activation(
-                    out=rows[g, h][:, t, :], in_=bank[:],
-                    func=ACT.Identity if h == INTEREST else ACT.Relu, bias=bias[:, col : col + 1],
+                    out=result_rows[g, kind][:, t, :],
+                    in_=bank[:],
+                    func=ACT.Identity if kind == INTEREST else ACT.Relu,
+                    bias=bias_columns[:, t, 1 if kind == INTEREST else 0, g : g + 1],
                 )
                 free_banks.append(b)
 
-        def interleave(g, h, half, engine):
-            c0, c1 = COLUMN_PIECES[h][half]
-            if (g, h) not in grouped:
-                grouped[g, h] = sbuf("grouped%d_%d" % (g, h), [P, 4 * N], BF16, tag="grouped", bufs=5)
+        def group(g, kind, half, engine):
+            if (g, kind) not in result_grouped:
+                result_grouped[g, kind] = sbuf(
+                    "result_grouped%d_%d" % (g, kind), [P, N, PACK], BF16, tag="result_grouped", bufs=GROUPED_BUFS
+                )
+            cols = COLUMNS[half]
             copy(
                 engine,
-                grouped[g, h][:, 4 * c0 : 4 * c1].rearrange("p (c i t) -> p c t i", i=4, t=4),
-                rows[g, h][:, :, c0:c1].rearrange("p t (c i) -> p c t i", i=4),
+                result_grouped[g, kind][:, cols, :].rearrange("p (c i) t -> p c t i", i=4),
+                result_rows[g, kind][:, :, cols].rearrange("p t (c i) -> p c t i", i=4),
             )
 
-        def quantize_result(g, h):
-            nc.vector.quantize_mx(out=words[g, h][:].bitcast(FP8X4), scales=scales[g, h][:], in_=grouped[g, h][:])
-
-        def second_stage(g, h, first, last):
-            for r in range(4):
-                if first:
-                    acc[h, r] = take_bank()
-                cols = slice(r * P, (r + 1) * P)
-                nc.tensor.matmul_mx(
-                    out=acc[h, r][1][:],
-                    lhsT=words[g, INTEREST][:, cols].bitcast(FP8X4), lhsT_scale=scales[g, INTEREST][:, cols],
-                    rhs=words[g, h][:].bitcast(FP8X4), rhs_scale=scales[g, h][:],
-                    start=first, stop=last,
-                )
-
-        def finish(h, r, engine):
-            b, bank = acc[h, r]
-            result = sbuf("result%d_%d" % (h, r), [P, N], F32, tag="result", bufs=4)
-            copy(engine, result[:], bank[:])
-            free_banks.append(b)
-            nc.sync.dma_start(out=out[r * P : (r + 1) * P, h * N : (h + 1) * N], in_=result[:])
-
-        def quantize_half(g, half):
-            c0, c1 = COLUMN_PIECES[1][half]
-            cols = slice(c0, c1)
-            nc.vector.quantize_mx(
-                out=words[g, 1][:, cols].bitcast(FP8X4), scales=scales[g, 1][:, cols],
-                in_=grouped[g, 1][:, 4 * c0 : 4 * c1],
+        def result_q(g, kind, part):
+            cols = COLUMNS[part]
+            quantize(
+                result_codes[g, kind][:, cols],
+                result_scales[g, kind][:, cols],
+                result_grouped[g, kind][:, cols, :].rearrange("p c t -> p (c t)"),
             )
 
-        def second_stage_half(g, half, first, last):
-            c0, c1 = COLUMN_PIECES[1][half]
-            ncols = slice(c0, c1)
-            for r in range(4):
-                if first:
-                    acc[1 + half, r] = take_bank()
-                cols = slice(r * P, (r + 1) * P)
+        def second(g, kind, part):
+            cols = COLUMNS[part]
+            for r in range(USER_TILES):
+                if g == 0:
+                    out_banks[kind, part, r] = take_bank()
+                user_cols = slice(r * P, (r + 1) * P)
                 nc.tensor.matmul_mx(
-                    out=acc[1 + half, r][1][:, : c1 - c0],
-                    lhsT=words[g, INTEREST][:, cols].bitcast(FP8X4), lhsT_scale=scales[g, INTEREST][:, cols],
-                    rhs=words[g, 1][:, ncols].bitcast(FP8X4), rhs_scale=scales[g, 1][:, ncols],
-                    start=first, stop=last,
+                    out=out_banks[kind, part, r][1][:, : cols.stop - cols.start],
+                    lhsT=result_codes[g, INTEREST][:, user_cols].bitcast(FP8X4),
+                    lhsT_scale=result_scales[g, INTEREST][:, user_cols],
+                    rhs=result_codes[g, kind][:, cols].bitcast(FP8X4),
+                    rhs_scale=result_scales[g, kind][:, cols],
+                    start=(g == 0), stop=(g == GROUPS - 1),
                 )
 
-        def finish_half(half, r, engine):
-            b, bank = acc[1 + half, r]
-            c0, c1 = COLUMN_PIECES[1][half]
-            per_store = TILES_PER_STORE[half]
+        def store(kind, part, r, engine):
+            cols = COLUMNS[part]
+            width = cols.stop - cols.start
+            per_store = N // width
             r0 = r - r % per_store
             if r == r0:
-                results[half, r0] = sbuf("result_half%d_%d" % (half, r0), [P, per_store, c1 - c0], F32)
-            copy(engine, results[half, r0][:, r - r0, :], bank[:, : c1 - c0])
+                out_tiles[kind, part, r0] = sbuf("out%d_%d_%d" % (kind, part, r0), [P, per_store, width], F32)
+            b, bank = out_banks[kind, part, r]
+            copy(engine, out_tiles[kind, part, r0][:, r - r0, :], bank[:, :width])
             free_banks.append(b)
             if r == r0 + per_store - 1:
-                dst = out[r0 * P : (r + 1) * P, N + c0 : N + c1]
-                nc.sync.dma_start(out=dst.rearrange("(r p) c -> p r c", p=P), in_=results[half, r0][:])
+                dst = out.rearrange("(p r) c -> p r c", r=USER_TILES)
+                c0 = kind * N + cols.start
+                nc.sync.dma_start(out=dst[:, r0 : r + 1, c0 : c0 + width], in_=out_tiles[kind, part, r0][:])
 
-        steps = {
-            "W": warm_up, "TK": group_traits_pass,
-            "QH": quantize_half, "OH": second_stage_half, "FH": finish_half,
-            "P": permute_pool, "B": make_bias, "T": transpose_users, "UQ": quantize_users,
-            "TI": group_traits, "TQ": quantize_traits, "S": first_stage, "IL": interleave,
-            "Q": quantize_result, "O": second_stage, "F": finish,
+        functions = {
+            "warm": warm, "bias": bias, "pool": pool, "users": users_step, "users_q": users_q,
+            "traits": traits_step, "traits_q": traits_q, "first": first, "group": group,
+            "result_q": result_q, "second": second, "store": store,
         }
-        for step in SCHEDULE:
-            steps[step[0]](*step[1:])
+        for step in STEPS:
+            functions[step[0]](*step[1:])

from contextlib import ExitStack

import concourse.mybir as mybir
from concourse.masks import make_identity

U, E, M, D, C = 512, 1024, 2048, 1024, 1024
FLOPS = 2 * (D * M * C + U * E * M + U * M * C)

F32 = mybir.dt.float32
BF16 = mybir.dt.bfloat16
I32 = mybir.dt.int32
U32 = mybir.dt.uint32
U8 = mybir.dt.uint8
FP8X4 = mybir.dt.float8_e4m3fn_x4
FP4X4 = mybir.dt.float4_e2m1fn_x4
ACT = mybir.ActivationFunctionType
ALU = mybir.AluOpType

P = 128
PACK = 4
N = 512
PASSES = 2
GROUPS = M // N
USER_TILES = U // P
BANKS = 8

GAIN_LO, GAIN_HI, INTEREST = 0, 1, 2
WHOLE = 2
COLUMNS = [slice(0, N // 2), slice(N // 2, N), slice(0, N)]
VECTOR, SCALAR = 0, 1

ROWS_BUFS = 9
GROUPED_BUFS = 5
TRAITS_BUFS = 2

STEPS = [
    ("warm", 7), ("bias",), ("warm", 5), ("pool", 0), ("first", 0, GAIN_LO), ("pool", 1), ("pool", 2),
    ("pool", 3), ("first", 1, GAIN_LO), ("group", 0, GAIN_LO, 0, VECTOR), ("group", 0, GAIN_LO, 1, VECTOR),
    ("traits", 0, 0, 2, VECTOR), ("traits", 0, 0, 3, VECTOR), ("traits", 0, 0, 0, VECTOR),
    ("group", 1, GAIN_LO, 0, VECTOR), ("traits", 0, 0, 1, VECTOR), ("first", 3, GAIN_LO), ("first", 2, GAIN_LO),
    ("traits", 0, 1, 1, VECTOR), ("traits_q", 0, 0, 1), ("traits", 0, 1, 3, VECTOR),
    ("traits", 0, 1, 2, VECTOR), ("traits", 0, 1, 0, VECTOR), ("first", 0, GAIN_HI),
    ("group", 3, GAIN_LO, 1, VECTOR), ("group", 3, GAIN_LO, 0, VECTOR), ("traits_q", 0, 1, 0),
    ("traits_q", 0, 1, 1), ("group", 1, GAIN_LO, 1, VECTOR), ("users", 1, SCALAR), ("first", 2, GAIN_HI),
    ("users", 0, SCALAR), ("group", 2, GAIN_LO, 0, VECTOR), ("traits", 1, 0, 2, VECTOR), ("traits_q", 0, 0, 0),
    ("result_q", 3, GAIN_LO, WHOLE), ("users_q", 1), ("traits", 1, 0, 0, VECTOR), ("first", 1, GAIN_HI),
    ("traits", 1, 1, 1, VECTOR), ("users_q", 0), ("traits", 1, 1, 0, VECTOR), ("first", 0, INTEREST),
    ("traits", 1, 0, 3, VECTOR), ("traits", 1, 1, 3, VECTOR), ("first", 1, INTEREST), ("traits_q", 1, 0, 1),
    ("traits", 1, 0, 1, VECTOR), ("traits_q", 1, 1, 0), ("traits", 1, 1, 2, VECTOR), ("traits_q", 1, 0, 0),
    ("group", 0, INTEREST, 1, VECTOR), ("traits_q", 1, 1, 1), ("group", 0, INTEREST, 0, VECTOR),
    ("first", 2, INTEREST), ("result_q", 1, GAIN_LO, WHOLE), ("group", 1, INTEREST, 1, VECTOR),
    ("first", 3, INTEREST), ("group", 2, GAIN_LO, 1, SCALAR), ("group", 1, INTEREST, 0, VECTOR),
    ("result_q", 0, INTEREST, WHOLE), ("group", 0, GAIN_HI, 0, VECTOR), ("group", 2, INTEREST, 0, VECTOR),
    ("group", 2, INTEREST, 1, VECTOR), ("result_q", 0, GAIN_LO, WHOLE), ("group", 3, INTEREST, 0, SCALAR),
    ("result_q", 0, GAIN_HI, 0), ("first", 3, GAIN_HI), ("second", 0, GAIN_LO, WHOLE),
    ("result_q", 1, INTEREST, WHOLE), ("group", 3, INTEREST, 1, VECTOR), ("result_q", 2, INTEREST, WHOLE),
    ("result_q", 2, GAIN_LO, WHOLE), ("result_q", 3, INTEREST, WHOLE), ("second", 1, GAIN_LO, WHOLE),
    ("second", 2, GAIN_LO, WHOLE), ("group", 2, GAIN_HI, 0, SCALAR), ("group", 1, GAIN_HI, 0, VECTOR),
    ("group", 1, GAIN_HI, 1, VECTOR), ("group", 3, GAIN_HI, 0, VECTOR), ("result_q", 1, GAIN_HI, 0),
    ("result_q", 2, GAIN_HI, 0), ("second", 3, GAIN_LO, WHOLE), ("store", GAIN_LO, WHOLE, 0, SCALAR),
    ("second", 0, GAIN_HI, 0), ("second", 1, GAIN_HI, 0), ("group", 0, GAIN_HI, 1, VECTOR),
    ("store", GAIN_LO, WHOLE, 1, SCALAR), ("result_q", 3, GAIN_HI, 0), ("second", 2, GAIN_HI, 0),
    ("result_q", 0, GAIN_HI, 1), ("group", 2, GAIN_HI, 1, VECTOR), ("second", 3, GAIN_HI, 0),
    ("store", GAIN_LO, WHOLE, 2, SCALAR), ("store", GAIN_LO, WHOLE, 3, SCALAR), ("second", 0, GAIN_HI, 1),
    ("result_q", 1, GAIN_HI, 1), ("second", 1, GAIN_HI, 1), ("store", GAIN_HI, 0, 0, VECTOR),
    ("result_q", 2, GAIN_HI, 1), ("group", 3, GAIN_HI, 1, SCALAR), ("store", GAIN_HI, 0, 1, SCALAR),
    ("second", 2, GAIN_HI, 1), ("store", GAIN_HI, 0, 2, SCALAR), ("result_q", 3, GAIN_HI, 1),
    ("store", GAIN_HI, 0, 3, VECTOR), ("second", 3, GAIN_HI, 1), ("store", GAIN_HI, 1, 0, SCALAR),
    ("store", GAIN_HI, 1, 1, VECTOR), ("store", GAIN_HI, 1, 2, SCALAR), ("store", GAIN_HI, 1, 3, VECTOR),
]


def tile_facility_location_gain_s12_kernel(
    tc, pool_words, pool_scales, cand_words, cand_scales, covered, users, traits, prior, out
):
    nc = tc.nc
    with ExitStack() as ctx:
        sb = ctx.enter_context(tc.tile_pool(name="sb", bufs=1))
        psum = ctx.enter_context(tc.psum_pool(name="psum", bufs=1))
        ctx.enter_context(tc.manual_schedule())

        def sbuf(name, shape, dtype, tag=None, bufs=1):
            return sb.tile(shape, dtype, name=name, tag=tag or name, bufs=bufs, align_bytes=64)

        def copy(engine, dst, src):
            if engine == VECTOR:
                nc.vector.tensor_copy(out=dst, in_=src)
            else:
                nc.scalar.copy(out=dst, in_=src)

        def quantize(codes, scales, values):
            nc.vector.quantize_mx(out=codes.bitcast(FP8X4), scales=scales, in_=values)

        free_banks = list(range(BANKS))
        taken = []

        def take_bank():
            b = free_banks.pop(0)
            taken.append(b)
            return b, psum.tile([P, N], F32, name="acc%d" % len(taken), tag="bank%d" % b)

        cand_codes = [sbuf("cand_codes%d" % h, [P, PASSES, 2 * N], U8) for h in range(2)]
        cand_scales_sb = sbuf("cand_scales_sb", [P, PASSES, C], U8)
        pool_raw_first = sbuf("pool_raw_first", [P, PASSES, 2 * N], U8)
        pool_raw_rest = sbuf("pool_raw_rest", [P, PASSES, 2 * (M - N)], U8)
        pool_raw = [pool_raw_first[:]] + [pool_raw_rest[:, :, 2 * N * j : 2 * N * (j + 1)] for j in range(GROUPS - 1)]
        pool_scales_raw = sbuf("pool_scales_raw", [P, PASSES, M], U8)
        pool_codes = [sbuf("pool_codes%d" % g, [P, PASSES, 2 * N], U8) for g in range(GROUPS)]
        pool_scales_sb = [sbuf("pool_scales_sb%d" % g, [P, PASSES, N], U8) for g in range(GROUPS)]
        vector_rows = sbuf("vector_rows", [P, N], BF16)
        vector_slots = sbuf("vector_slots", [P, N], F32)
        bias_columns = sbuf("bias_columns", [P, PACK, 2, GROUPS], F32)
        identity = sbuf("identity", [P, P], F32)
        table_out = sbuf("table_out", [P, 2], F32)
        zero_codes = sbuf("zero_codes", [P, N // 2], U32)
        zero_scales = sbuf("zero_scales", [P, N // 2], U8)
        users_raw = sbuf("users_raw", [P, USER_TILES * E], BF16)
        users_grouped = [sbuf("users_grouped%d" % k, [P, PACK * U], BF16) for k in range(PASSES)]
        users_codes = [sbuf("users_codes%d" % k, [P, U], U32) for k in range(PASSES)]
        users_scales = [sbuf("users_scales%d" % k, [P, U], U8) for k in range(PASSES)]
        traits_raw, traits_codes, traits_scales = {}, {}, {}
        for pair in range(GROUPS // 2):
            for k in range(PASSES):
                traits_raw[pair, k] = sbuf("traits_raw%d_%d" % (pair, k), [P, PACK, 2 * N], BF16)
                traits_codes[pair, k] = sbuf("traits_codes%d_%d" % (pair, k), [P, PACK, 2 * P], U32)
                traits_scales[pair, k] = sbuf("traits_scales%d_%d" % (pair, k), [P, PACK, 2 * P], U8)
        result_codes, result_scales = {}, {}
        for g in range(GROUPS):
            for kind in (GAIN_LO, GAIN_HI, INTEREST):
                result_codes[g, kind] = sbuf("result_codes%d_%d" % (g, kind), [P, N], U32)
                result_scales[g, kind] = sbuf("result_scales%d_%d" % (g, kind), [P, N], U8)
        traits_grouped, result_rows, result_grouped, out_banks, out_tiles = {}, {}, {}, {}, {}

        def load_fp4_words(dst, words, first_column):
            src = words.bitcast(I32).rearrange("k p n -> p k n")
            width = dst.shape[2] // 4
            nc.sync.dma_start(out=dst[:].bitcast(I32), in_=src[:, :, first_column // 2 : first_column // 2 + width])

        def load_scale_rows(dst, scales):
            src = scales.bitcast(I32).rearrange("k (q r) n -> r q k n", r=4)
            for r in range(4):
                nc.sync.dma_start(out=dst[r:P:32].bitcast(I32), in_=src[r])

        def load_traits(pair, k):
            src = traits[k * N : (k + 1) * N, pair * 2 * N : (pair + 1) * 2 * N]
            nc.sync.dma_start(out=traits_raw[pair, k][:], in_=src.rearrange("(p j) m -> p j m", j=PACK))

        nc.vector.memset(pool_scales_raw[:].bitcast(I32), 0)
        nc.vector.memset(cand_scales_sb[:].bitcast(I32), 0)
        nc.gpsimd.memset(vector_slots[:], 0.0)
        make_identity(nc, identity[:])
        quantize(zero_codes[:], zero_scales[:], vector_slots[:].bitcast(BF16))
        nc.scalar.activation(out=table_out[:], in_=vector_slots[:, 0:2], func=ACT.Relu)

        nc.sync.dma_start(out=vector_rows[0:4, :], in_=covered.rearrange("(g m) -> g m", g=GROUPS))
        nc.sync.dma_start(out=vector_rows[32:36, :], in_=prior.rearrange("(g m) -> g m", g=GROUPS))
        load_fp4_words(cand_codes[0], cand_words, 0)
        load_fp4_words(pool_raw_first, pool_words, 0)
        load_scale_rows(pool_scales_raw, pool_scales)
        load_scale_rows(cand_scales_sb, cand_scales)
        load_fp4_words(pool_raw_rest, pool_words, N)
        load_traits(0, 0)
        load_traits(0, 1)
        load_fp4_words(cand_codes[1], cand_words, N)
        nc.sync.dma_start(out=users_raw[:], in_=users.rearrange("(p r) e -> p (r e)", r=USER_TILES))
        load_traits(1, 0)
        load_traits(1, 1)

        def warm(count):
            b, bank = take_bank()
            for i in range(count):
                nc.tensor.matmul_mx(
                    out=bank[:, : N // 2],
                    lhsT=zero_codes[:, :P].bitcast(FP8X4), lhsT_scale=zero_scales[:, :P],
                    rhs=zero_codes[:].bitcast(FP8X4), rhs_scale=zero_scales[:],
                    start=True, stop=True,
                )
            free_banks.append(b)

        def bias():
            by_slot = vector_slots[:].rearrange("g (t b i) -> g t b i", t=PACK, i=8)
            by_item = vector_rows[:].rearrange("g (b t i) -> g t b i", t=PACK, i=8)
            nc.vector.tensor_scalar(out=by_slot[0:4], in0=by_item[0:4], scalar1=-1.0, scalar2=None, op0=ALU.mult)
            nc.vector.tensor_copy(out=by_slot[32:36], in_=by_item[32:36])
            b, bank = take_bank()
            for t in range(PACK):
                cols = slice(t * P, (t + 1) * P)
                nc.tensor.transpose(bank[:, cols], vector_slots[:, cols], identity[:])
            src = bank[:].rearrange("p (t v g) -> p t v g", t=PACK, g=32)
            nc.vector.tensor_copy(out=bias_columns[:], in_=src[:, :, 0:2, 0:GROUPS])
            free_banks.append(b)

        def pool(g):
            for dst, src, w in (
                (pool_codes[g][:], pool_raw[g], 4),
                (pool_scales_sb[g][:], pool_scales_raw[:, :, g * N : (g + 1) * N], 2),
            ):
                nc.vector.tensor_copy(
                    out=dst.bitcast(I32).rearrange("p k (t b w) -> p k t b w", t=PACK, w=w),
                    in_=src.bitcast(I32).rearrange("p k (b t w) -> p k t b w", t=PACK, w=w),
                )

        def users_step(k, engine):
            pairs = users_raw[:].bitcast(F32)
            dst = users_grouped[k][:].bitcast(F32).rearrange("p (r x u) -> p r x u", r=USER_TILES, u=2)
            for r0 in range(0, USER_TILES, 2):
                b, bank = take_bank()
                for r in (r0, r0 + 1):
                    w0 = (r * E + k * N) // 2
                    for u in range(2):
                        col = (2 * (r - r0) + u) * P
                        nc.tensor.transpose(bank[:, col : col + P], pairs[:, w0 + u : w0 + N // 2 : 2], identity[:])
                copy(engine, dst[:, r0 : r0 + 2], bank[:].rearrange("p (r u x) -> p r x u", r=2, u=2))
                free_banks.append(b)

        def users_q(k):
            quantize(users_codes[k][:], users_scales[k][:], users_grouped[k][:])

        def traits_step(pair, k, t, engine):
            if (pair, k) not in traits_grouped:
                traits_grouped[pair, k] = sbuf(
                    "traits_grouped%d_%d" % (pair, k), [P, PACK, 2 * N], BF16, tag="traits_grouped", bufs=TRAITS_BUFS
                )
            copy(
                engine,
                traits_grouped[pair, k][:, t, :].rearrange("p (b h i j) -> p b h j i", h=2, i=4, j=PACK),
                traits_raw[pair, k][:].rearrange("p j (b t h i) -> p t b h j i", t=PACK, h=2, i=4)[:, t],
            )

        def traits_q(pair, k, half):
            slots = slice(2 * half, 2 * half + 2)
            quantize(
                traits_codes[pair, k][:, slots, :].rearrange("p t c -> p (t c)"),
                traits_scales[pair, k][:, slots, :].rearrange("p t c -> p (t c)"),
                traits_grouped[pair, k][:, slots, :].rearrange("p t c -> p (t c)"),
            )

        def first(g, kind):
            result_rows[g, kind] = sbuf("result_rows%d_%d" % (g, kind), [P, PACK, N], BF16, tag="result_rows", bufs=ROWS_BUFS)
            for t in range(PACK):
                b, bank = take_bank()
                for k in range(PASSES):
                    if kind == INTEREST:
                        cols = slice((g % 2) * P, (g % 2 + 1) * P)
                        lhsT = traits_codes[g // 2, k][:, t, cols].bitcast(FP8X4)
                        lhsT_scale = traits_scales[g // 2, k][:, t, cols]
                        rhs, rhs_scale = users_codes[k][:].bitcast(FP8X4), users_scales[k][:]
                    else:
                        lhsT = pool_codes[g][:, k, 2 * t * P : 2 * (t + 1) * P].bitcast(FP4X4)
                        lhsT_scale = pool_scales_sb[g][:, k, t * P : (t + 1) * P]
                        rhs = cand_codes[kind][:, k, :].bitcast(FP4X4)
                        rhs_scale = cand_scales_sb[:, k, kind * N : (kind + 1) * N]
                    nc.tensor.matmul_mx(
                        out=bank[:], lhsT=lhsT, lhsT_scale=lhsT_scale, rhs=rhs, rhs_scale=rhs_scale,
                        start=(k == 0), stop=(k == PASSES - 1),
                    )
                nc.scalar.activation(
                    out=result_rows[g, kind][:, t, :],
                    in_=bank[:],
                    func=ACT.Identity if kind == INTEREST else ACT.Relu,
                    bias=bias_columns[:, t, 1 if kind == INTEREST else 0, g : g + 1],
                )
                free_banks.append(b)

        def group(g, kind, half, engine):
            if (g, kind) not in result_grouped:
                result_grouped[g, kind] = sbuf(
                    "result_grouped%d_%d" % (g, kind), [P, N, PACK], BF16, tag="result_grouped", bufs=GROUPED_BUFS
                )
            cols = COLUMNS[half]
            copy(
                engine,
                result_grouped[g, kind][:, cols, :].rearrange("p (c i) t -> p c t i", i=4),
                result_rows[g, kind][:, :, cols].rearrange("p t (c i) -> p c t i", i=4),
            )

        def result_q(g, kind, part):
            cols = COLUMNS[part]
            quantize(
                result_codes[g, kind][:, cols],
                result_scales[g, kind][:, cols],
                result_grouped[g, kind][:, cols, :].rearrange("p c t -> p (c t)"),
            )

        def second(g, kind, part):
            cols = COLUMNS[part]
            for r in range(USER_TILES):
                if g == 0:
                    out_banks[kind, part, r] = take_bank()
                user_cols = slice(r * P, (r + 1) * P)
                nc.tensor.matmul_mx(
                    out=out_banks[kind, part, r][1][:, : cols.stop - cols.start],
                    lhsT=result_codes[g, INTEREST][:, user_cols].bitcast(FP8X4),
                    lhsT_scale=result_scales[g, INTEREST][:, user_cols],
                    rhs=result_codes[g, kind][:, cols].bitcast(FP8X4),
                    rhs_scale=result_scales[g, kind][:, cols],
                    start=(g == 0), stop=(g == GROUPS - 1),
                )

        def store(kind, part, r, engine):
            cols = COLUMNS[part]
            width = cols.stop - cols.start
            per_store = N // width
            r0 = r - r % per_store
            if r == r0:
                out_tiles[kind, part, r0] = sbuf("out%d_%d_%d" % (kind, part, r0), [P, per_store, width], F32)
            b, bank = out_banks[kind, part, r]
            copy(engine, out_tiles[kind, part, r0][:, r - r0, :], bank[:, :width])
            free_banks.append(b)
            if r == r0 + per_store - 1:
                dst = out.rearrange("(p r) c -> p r c", r=USER_TILES)
                c0 = kind * N + cols.start
                nc.sync.dma_start(out=dst[:, r0 : r + 1, c0 : c0 + width], in_=out_tiles[kind, part, r0][:])

        functions = {
            "warm": warm, "bias": bias, "pool": pool, "users": users_step, "users_q": users_q,
            "traits": traits_step, "traits_q": traits_q, "first": first, "group": group,
            "result_q": result_q, "second": second, "store": store,
        }
        for step in STEPS:
            functions[step[0]](*step[1:])
